import numpy as np, ml_dtypes
CORES = [36,164,52,180,100,228,116,244]
N = 8
BF = ml_dtypes.bfloat16
def gentries(a):
    return np.ascontiguousarray(a.reshape(8, 16, -1).transpose(0, 2, 1)).reshape(8, -1)
def gtable(e):
    e = np.asarray(e); return np.ascontiguousarray(e.reshape(8, -1, 16).transpose(0, 2, 1)).reshape(128, -1).astype(np.int32)
W, F, C, K, TV, R = 2048, 1024, 256, 3, 4, 8
def num(l, b, t):
    return ((l * b >> 5) + l + 37 * b + 77 * t) & (F - 1)
def parts(rng):
    x = rng.integers(0, 16, (N, 8, 16, W)); fa = rng.integers(0, W, (N, 8, 16, F))
    l = rng.integers(0, W, (N, 8, K, C)); u = np.stack([rng.integers(-1, k, (N, 8, C)) for k in range(K)], axis=2)
    return x, fa, l, u, rng.integers(0, W, (N, 8, C)), rng.integers(36, 76, (N, 8, K)), rng.integers(0, 16, (N, 8, 16))
def pack(x, fa, l, u, e, th, w):
    return {"xs": np.ascontiguousarray(x.reshape(N, 128, W)).astype(np.float32).astype(BF), "fa": np.ascontiguousarray(fa.reshape(N, 128, F)).astype(np.int32),
            "lc": np.stack([gtable(a.reshape(8, -1)) for a in l]), "up": np.stack([gtable(a.reshape(8, -1)) for a in u]), "ex": np.stack([gtable(a) for a in e]),
            "th": np.ascontiguousarray(th).astype(np.int32), "wt": np.ascontiguousarray(w.reshape(N, 128, 1)).astype(np.int32)}
def setup_inputs(rng):
    return pack(*parts(rng))
def setup_inputs_spread(rng):
    x, fa, l, u, e, th, w = parts(rng)
    x = np.minimum((np.exp2(4 * rng.random((N, 8, 1, W))) * rng.random((N, 8, 16, W))).astype(np.int64), 15)
    a = rng.choice(np.array([1, 2, 4]), (N, 8, 1, 1))
    fa = np.minimum((W * rng.random(fa.shape) ** a).astype(np.int64), W - 1); l = np.minimum((W * rng.random(l.shape) ** a).astype(np.int64), W - 1)
    e = np.minimum((W * rng.random(e.shape) ** a[..., 0]).astype(np.int64), W - 1)
    th = np.minimum(np.exp2(8 * rng.random(th.shape)).astype(np.int64) - 1, 255); w = np.minimum(np.exp2(4 * rng.random(w.shape)).astype(np.int64) - 1, 15)
    return pack(x, fa, l, u, e, th, w)
def setup_inputs_ends(rng):
    x, fa, l, u, e, th, w = parts(rng)
    kind = rng.integers(0, 4, (N, 8, 1, W)); x = np.where(kind == 0, 0, np.where(kind == 1, 15, 15 * rng.integers(0, 2, x.shape)))
    x[..., 0] = 0; x[..., W - 1] = 15
    kind = rng.integers(0, 4, (N, 8, 1, F)); end = (W - 1) * rng.integers(0, 2, fa.shape)
    fa = np.where(kind == 0, 0, np.where(kind == 1, W - 1, np.where((kind == 2) | (rng.random(fa.shape) < 0.5), end, fa)))
    l = np.where(rng.random(l.shape) < 0.85, (W - 1) * rng.integers(0, 2, l.shape), l)
    e = np.where(rng.random(e.shape) < 0.85, (W - 1) * rng.integers(0, 2, e.shape), e)
    u = np.where(rng.random(u.shape) < 0.6, -1, np.arange(K)[:, None] - 1)
    th = 255 * rng.integers(0, 2, th.shape); th[:, 0, 0] = 0; th[:, 7] = 255
    w = 15 * rng.integers(0, 2, w.shape); w[:, 0] = 0; w[:, 7] = 15
    e[:, :, C - 1] = W - 1; l[:, :, 0, C - 1] = W - 1; l[:, :, 1, C - 1] = 0; u[:, :, 1, C - 1] = -1; u[:, :, K - 1, 0] = K - 2
    n0, n1 = num(W - 1, W - 1, 0), num(0, W - 1, 0)
    for g in (3, 7):
        x[:, g, :, 1:4] = 0; fa[:, g, :, n0] = rng.integers(0, 4, (N, 16)); fa[:, g, 0, n0] = 3; fa[:, g, 1, n0] = 0; fa[:, g, :, n1] = W - 1
    return pack(x, fa, l, u, e, th, w)
def setup_inputs_corners(rng):
    x, fa, l, u, e, th, w = parts(rng); k = np.arange(K)[:, None]
    for s in range(N):
        for g in range(8):
            m = (g + s) % 8
            if m == 0: u[s, g] = k - 1; th[s, g] = 255; th[s, g, 0] = 0
            if m == 1: u[s, g] = k - 1; th[s, g] = 255
            if m == 2: u[s, g] = -1; th[s, g] = rng.choice(np.array([0, 255]), K); w[s, g] = 0
            if m == 3: u[s, g] = k - 1; th[s, g] = 255; th[s, g, K - 1] = 0; w[s, g] = 15
            if m == 4: u[s, g] = np.minimum(k - 1, 0)
            if m == 5: x[s, g] = rng.integers(0, 16, W); th[s, g] = rng.choice(np.array([0, 1, 16, 17, 32]), K)
            if m == 6: x[s, g] = x[s, g][:, rng.integers(0, 8, W)]
            if m == 7:
                fa[s, g] = fa[s, g, :1].copy(); fa[s, g, :, ::4] = rng.choice(np.array([0, W - 1, W // 2, W // 2 + 1]), (16, F // 4))
                e[s, g] = rng.choice(np.array([0, W - 1, W // 2, 1]), C); l[s, g, ::2] = e[s, g]; th[s, g] = rng.integers(60, 110, K)
    return pack(x, fa, l, u, e, th, w)
def setup_inputs_crowd(rng):
    x, fa, l, u, e, th, w = parts(rng)
    for s in (0, 2):
        for g in range(8):
            x[s, g, :, :8] = 0; o = np.argsort(np.sum(x[s, g], axis=0)); e[s, g] = rng.choice(o[W // 2:], C); one = s == 2 and g == 7
            if one: l[s, g, K - 1, C - 1] = e[s, g, C - 1]; u[s, g, K - 1, C - 1] = -1; th[s, g] = 1
            n = num(l[s, g], e[s, g], 0)
            fa[s, g][:, n.reshape(-1)] = rng.integers(0, 8, (16, K * C))
            if one: fa[s, g, int(rng.integers(0, 16)), n[K - 1, C - 1]] = e[s, g, C - 1]
    for s in range(1, N, 2):
        for g in (0, 4):
            e[s, g] = int(e[s, g, 0]); l[s, g] = l[s, g, :, :1].copy(); u[s, g] = u[s, g, :, :1].copy()
        l[s, 4, :, C - 1] = rng.integers(0, W, K)
    if N > 5: th[5] = 255
    return pack(x, fa, l, u, e, th, w)
def setup_inputs_brink(rng):
    x, fa, l, u, e, th, w = parts(rng); al = np.arange(W); odd = np.arange(1, C, 2)
    pq = np.array([[3, 21], [21, 3], [5, 19], [19, 5], [7, 9], [9, 7]])
    for s in range(N):
        for g in range(8):
            m = (g + s) % 8
            if m < 3: u[s, g] = np.arange(K)[:, None] - 1; th[s, g] = 255
            if m == 0:
                used = np.zeros(F, bool)
                for i in range(C):
                    n = num(al, int(e[s, g, i]), 0); room = np.flatnonzero(~used[n])
                    if len(room) == 0: e[s, g, i] = 0; n = num(al, 0, 0); room = np.flatnonzero(~used[n])
                    v = int(room[int(rng.integers(0, len(room)))]); l[s, g, 0, i] = v; used[n[v]] = True
            if m == 1:
                lo = 512 * int(rng.integers(0, W // 512)); d = int(rng.integers(0, 512)); v = lo + d
                fa[s, g] = lo + rng.integers(0, 512, (16, F)); x[s, g, :, v] = 15
                e[s, g, C - 1] = v; l[s, g, 0, C - 1] = v; n = num(v, v, 0)
                fa[s, g, :15, n] = lo + ((d + rng.integers(1, 512, 15)) & 511); fa[s, g, 15, n] = v
            if m == 2:
                j = pq[rng.integers(0, 6, len(odd))]; l[s, g, 0, odd] = W - j[:, 0]; e[s, g, odd] = W - j[:, 1]
            if m == 3 or m == 4:
                o = rng.permutation(W)[:192]; x[s, g][:, o[:128]] = 0; x[s, g][rng.integers(0, 16, 64), o[64:128]] = 1; x[s, g][:, o[128:]] = 15
                e[s, g, odd] = rng.choice(o[128:], len(odd)); u[s, g][:, odd] = -1
                n = num(l[s, g][:, odd], e[s, g, odd], 0).reshape(-1); c = rng.choice(o[:64], (16, F))
                if m == 4:
                    hit = rng.random((16, F)) < 0.25; hit[0] = False; hit[15] = True
                    c = np.where(hit, rng.choice(o[64:128], (16, F)), c)
                fa[s, g][:, n] = c[:, n]
                th[s, g] = np.resize(np.array([240, 241, 239]) if m == 3 else np.array([240, 239, 241]), K)
    return pack(x, fa, l, u, e, th, w)
def check_inputs(d):
    bad = []
    for k, lo, hi in (("xs", 0, 15), ("fa", 0, W - 1), ("lc", 0, W - 1), ("up", -1, K - 2), ("ex", 0, W - 1), ("th", 0, 255), ("wt", 0, 15)):
        v = np.asarray(d[k]).astype(np.float32)
        if not (np.min(v) >= lo and np.max(v) <= hi): bad.append("range of " + k)
        if k == "xs" and np.any(v != np.floor(v)): bad.append("whole numbers in xs")
    u = np.stack([gentries(a) for a in np.asarray(d["up"])]).reshape(N, 8, K, C)
    if np.any(u > np.arange(K)[:, None] - 1): bad.append("inputs in up that are not rows before")
    return bad
def reference(xs, fa, lc, up, ex, th, wt):
    X = xs.astype(np.float32).astype(np.int32).reshape(N, 8, 16, W); FC = fa.astype(np.int64).reshape(N, 8, 16, F)
    L = np.stack([gentries(a) for a in lc]).astype(np.int64).reshape(N, 8, K, C); U = np.stack([gentries(a) for a in up]).astype(np.int64).reshape(N, 8, K, C)
    E = np.stack([gentries(a) for a in ex]).astype(np.int64); H = th.astype(np.int64); V = wt.astype(np.int64).reshape(N, 8, 16, 1)
    A = np.zeros(N, np.int64)
    for t in range(TV):
        deaths = np.zeros(N, np.int64)
        for s in range(N):
            r = (s - t) % N; l, u, x = L[r], U[r], X[s]
            beta = np.zeros((8, K + 1, C), np.int64); beta[:, 0] = E[s]
            live = np.ones((8, K + 1, C), bool); y = np.zeros((8, 16, C), np.int32)
            for k in range(K):
                j = u[:, k:k + 1] + 1
                b = np.take_along_axis(beta, j, 1)[:, 0]; ok = np.take_along_axis(live, j, 1)[:, 0]
                c = np.take_along_axis(FC[s], num(l[:, k], b, t)[:, None, :], 2)
                q = np.maximum(np.take_along_axis(x, l[:, k:k + 1], 2), np.take_along_axis(x, b[:, None, :], 2))
                v = np.take_along_axis(x, np.ascontiguousarray(c.transpose(0, 2, 1)).reshape(8, 1, 16 * C), 2).reshape(8, 16, C, 16)
                dist = np.add.reduce(np.abs(v - q[..., None]), axis=1)
                m = np.argmin(dist, axis=2)
                ok = ok & (np.min(dist, axis=2) < H[s][:, k:k + 1] + A[s])
                beta[:, k + 1] = np.take_along_axis(c, m[:, None, :], 1)[:, 0]; live[:, k + 1] = ok
                y = np.maximum(y, np.where(ok[:, None, :], np.take_along_axis(x, beta[:, k + 1:k + 2], 2), 0))
            place = R * np.arange(C) + (np.add.reduce(V[s] * y, axis=1) & (R - 1))
            np.put_along_axis(x, np.repeat(place[:, None, :], 16, axis=1), y, 2)
            last = np.zeros((8, C), np.int64)
            for k in range(K):
                p = np.take_along_axis(beta, last[:, None, :], 1)[:, 0]; dead = ~live[:, k + 1]
                l[:, k] = np.where(dead, ((l[:, k] * p >> 5) + 37 * p + k) & (W - 1), l[:, k])
                u[:, k] = np.where(dead, last - 1, u[:, k])
                last = np.where(dead, last, k + 1)
            deaths[s] = np.count_nonzero(~live)
        A = deaths & 31
    return {"yl": np.stack([gtable(a.reshape(8, -1)) for a in L]).astype(np.float32), "yi": np.stack([gtable(a.reshape(8, -1)) for a in U]).astype(np.float32),
            "yx": X.reshape(N, 128, W).astype(np.float32).astype(BF)}

@@ -1,0 +1,502 @@
+from concourse.mybir import dt, AluOpType, AxisListType, ActivationFunctionType
+
+OP = AluOpType
+ACT = ActivationFunctionType
+NV, NR, PAD, FW = 4, 3, 32, 1264
+BIG = 16777216.0
+ROT = 864
+
+SCRATCH = {}
+
+
+def _decl(where, dtype, names, n, rows=128):
+    for nm in names.split():
+        SCRATCH[nm] = (where, [rows, n], dtype)
+
+
+_decl("sbuf", "bfloat16", "X", 2080)
+_decl("sbuf", "int32", "FA", 2 * FW)
+_decl("sbuf", "float32", "C CT", 256)
+_decl("sbuf", "uint16", "CTu", 256)
+_decl("sbuf", "bfloat16", "qq yy y0 y01", 256)
+_decl("sbuf", "bfloat16", "Q4 z0 z1 z2 z3", 1024)
+_decl("psum", "float32", "q4ps", 1024)
+_decl("psum", "float32", "CV MS D0 D1 D2 D3", 512)
+_decl("sbuf", "float32", "SC0 SC1 SC2 SC3 RST", 64)
+_decl("sbuf", "int32", "EXi", 64)
+_decl("sbuf", "uint16", "EXu", 64)
+_decl("sbuf", "int32", "lci upi", 48)
+_decl("sbuf", "int32", "thi", 3, 8)
+_decl("sbuf", "float32", "thf", 3, 8)
+_decl("sbuf", "float32", "tsel", 128, 8)
+_decl("sbuf", "bfloat16", "MK", 256, 1)
+_decl("sbuf", "int32", "wti ai ai2 pi pg p15", 1)
+_decl("sbuf", "float32", "wtf cnt af par p8 p15f", 1)
+_decl("sbuf", "float32", "thk Tk", 3)
+_decl("sbuf", "float32", "nc", 8)
+_decl("sbuf", "float32", "onef D160", 160)
+_decl("sbuf", "bfloat16", "Ev Od", 160)
+_decl("sbuf", "float32", "W", 144)
+_decl("sbuf", "bfloat16", "W65 SW", 144)
+_decl("sbuf", "float32", "I32", 128)
+_decl("sbuf", "bfloat16", "IB oneb", 128)
+_decl("sbuf", "int32", "exi b128 base z32 nn t2 bi rz rz2 si sm sa", 16)
+_decl("sbuf", "uint16", "Eu nu bu wu", 16)
+_decl("sbuf", "bfloat16", "eh el bh bl lt", 16)
+_decl("sbuf", "float32", "mone Ep Er Es M Mu t1 yo n1 u1 w1 n2 u2 w2 s20 s21 nE sB g1 g2 ga gb px P1p P1r P2r p2", 16)
+_decl("sbuf", "int32", "NW", 32)
+_decl("sbuf", "float32", "df dd", 32)
+_decl("sbuf", "bfloat16", "lv Lh Ll", 48)
+_decl("sbuf", "uint16", "Lu yu", 48)
+_decl("sbuf", "float32", "LA LS", 48)
+_decl("sbuf", "int32", "K B", 48)
+_decl("sbuf", "bfloat16", "XL", 768)
+_decl("sbuf", "float32", "land_0 land_1 land_2", 160)
+_decl("sbuf", "float32", "src_0 src_1 src_2", 128)
+
+SEMAPHORES = ["cv", "cs", "cp", "cg", "ls", "dfa", "dfw", "dx", "dlc", "dup", "dex", "dth", "dwt", "dout"]
+SEMAPHORES += ["ar%d_%d" % (t, k) for t in range(1, 5) for k in range(NR)]
+
+
+def rank_program(g, core, T, topo):
+    rank = T.rank_of(core)
+    if rank is None:
+        return
+    n_ranks = len(T.cores)
+    QUEUE = {"v": g.vector, "s": g.scalar, "p": g.tensor, "g": g, "y": g.sync}
+    count = {"v": 0, "s": 0, "p": 0, "g": 0}
+    known = {q: {} for q in QUEUE}
+    snap, lastw, readers, sent = {}, {}, {}, [0]
+
+    def need(q, sem, val):
+        if known[q].get(sem, 0) >= val:
+            return
+        QUEUE[q].wait_ge(T.sem[sem], val)
+        for s_, v_ in snap.get((sem, val), {}).items():
+            if known[q].get(s_, 0) < v_:
+                known[q][s_] = v_
+        known[q][sem] = val
+
+    def before(q, r, w):
+        deps = {}
+
+        def add(d):
+            if deps.get(d[0], 0) < d[1]:
+                deps[d[0]] = d[1]
+        for b in r:
+            if b in lastw:
+                add(lastw[b])
+        for b in w:
+            if b in lastw and not (lastw[b][2] == q and q == "p"):
+                add(lastw[b])
+            for d in readers.get(b, ()):
+                if d[2] != q:
+                    add(d)
+        for sem in sorted(deps, key=lambda s_: -len(snap.get((s_, deps[s_]), {}))):
+            need(q, sem, deps[sem])
+
+    def after(q, sem, val, r, w):
+        d = (sem, val, q)
+        for b in r:
+            readers.setdefault(b, []).append(d)
+        for b in w:
+            lastw[b] = d
+            readers[b] = []
+        snap[(sem, val)] = dict(known[q])
+
+    def op(q, fn, r, w):
+        r, w = r.split(), w.split()
+        before(q, r, w)
+        ins = fn(QUEUE[q])
+        count[q] += 1
+        ins.then_inc(T.sem["c" + q], 1)
+        after(q, "c" + q, count[q], r, w)
+
+    def dma(q, out, in_, sem, total, r, w):
+        r, w = r.split(), w.split()
+        before(q, r, w)
+        QUEUE[q].dma_start(out=out, in_=in_).then_inc(T.sem[sem], 16)
+        after(q, sem, total, r, w)
+
+    def tt(o, a, b, f, r, w):
+        op("v", lambda e: e.tensor_tensor(out=o, in0=a, in1=b, op=f), r, w)
+
+    def ts(o, a, s1, s2, f0, f1, r, w):
+        if s2 is None:
+            op("v", lambda e: e.tensor_scalar(out=o, in0=a, scalar1=s1, scalar2=None, op0=f0), r, w)
+        else:
+            op("v", lambda e: e.tensor_scalar(out=o, in0=a, scalar1=s1, scalar2=s2, op0=f0, op1=f1), r, w)
+
+    def cp(o, a, r, w):
+        op("v", lambda e: e.tensor_copy(out=o, in_=a), r, w)
+
+    def fill(o, c, w):
+        op("v", lambda e: e.memset(o, c), "", w)
+
+    def act(o, a, f, r, w, bias=0.0, scale=1.0):
+        op("s", lambda e: e.activation(out=o, in_=a, func=f, bias=bias, scale=scale), r, w)
+
+    def mms(lst, r, w):
+        def fn(e):
+            ins = None
+            for (o, a, b, st, sp) in lst:
+                ins = e.matmul(out=o, lhsT=a, rhs=b, start=st, stop=sp)
+            return ins
+        op("p", fn, r, w)
+
+    def kk(nm, k):
+        return T[nm][:, 16 * k:16 * k + 16]
+
+    Xw = T.X[:, 0:2080]
+
+    dma("y", T.exi[:], T.ex[:], "dex", 16, "", "exi")
+    dma("s", T.lci[:], T.lc[:], "dlc", 16, "", "lci")
+    it = [0]
+
+    def lfa(rows, src, blk):
+        for (a, b, c) in ((0, ROT, 1024), (1024 - ROT, 0, ROT)):
+            q = "ys"[it[0] % 2]
+            it[0] += 1
+            dma(q, T.FA[rows, blk * FW + a:blk * FW + a + c - b], T.fa[src, b:c], "dfa", 288, "", "FA%d" % it[0])
+    lfa(slice(0, 128), slice(0, 128), 0)
+    for G in range(8):
+        o = G ^ 1
+        lfa(slice(16 * G, 16 * G + 16), slice(16 * o, 16 * o + 16), 1)
+    FAtok = " ".join("FA%d" % (i + 1) for i in range(it[0]))
+    dma("y", T.X[:, PAD:PAD + 2048], T.xs[:], "dx", 16, "", "X")
+    dma("s", T.upi[:], T.up[:], "dup", 16, "", "upi")
+    dma("s", T.thi[:], T.th[:], "dth", 16, "", "thi")
+    dma("s", T.wti[:], T.wt[:], "dwt", 16, "", "wti")
+
+    fill(T.onef[:], 1.0, "onef")
+    op("g", lambda e: e.iota(T.pi[:], [[0, 1]], 0, 1), "", "pi")
+
+    def aff(o, a, pat, f, base, cm, r, w):
+        op("g", lambda e: e.affine_select(o, a, pat, f, 0.0, base, cm), r, w)
+    aff(T.D160[:], T.onef[:], [[-1, 160]], OP.is_equal, 16, 1, "onef", "D160")
+    op("g", lambda e: e.iota(T.EXi[:], [[16, 16], [0, 4]], 0, 0), "", "EXi")
+    aff(T.I32[:], T.onef[:, 0:128], [[-1, 128]], OP.is_equal, 0, 1, "onef", "I32")
+    op("g", lambda e: e.iota(T.MK[0:1, :], [[4096, 4], [0, 16], [16384, 4]], 0, 0,
+                             allow_small_or_imprecise_dtypes=True), "", "MK")
+    aff(T.W[:], T.onef[:, 0:144], [[-16, 9], [0, 16]], OP.is_ge, 0, 1, "onef", "W")
+    aff(T.W[:], T.W[:], [[16, 9], [0, 16]], OP.is_ge, 15, -1, "W", "W")
+    aff(T.W[:], T.W[:], [[0, 9], [1, 16]], OP.is_equal, -15, 0, "W", "W")
+    aff(T.RST[:], T.onef[:, 0:64], [[0, 16], [1, 4]], OP.is_equal, 0, 0, "onef", "RST")
+    op("g", lambda e: e.iota(T.b128[:], [[128, 16]], PAD, 0), "", "b128")
+    aff(T.tsel[:], T.onef[0:8, 0:128], [[1, 128]], OP.is_ge, 0, -16, "onef", "tsel")
+    aff(T.tsel[:], T.tsel[:], [[-1, 128]], OP.is_ge, 15, 16, "tsel", "tsel")
+
+    fill(T.FA[:, 1024:FW], 0, "FAx0")
+    fill(T.FA[:, FW + 1024:2 * FW], 0, "FAx1")
+    fill(T.X[:, 0:PAD], 0.0, "Xpad")
+    fill(T.oneb[:], 1.0, "oneb")
+    ts(T.pg[:], T.pi[:], 4, 1, OP.arith_shift_right, OP.bitwise_and, "pi", "pg")
+    ts(T.p15[:], T.pi[:], 15, None, OP.bitwise_and, None, "pi", "p15")
+    cp(T.par[:], T.pg[:], "pg", "par")
+    cp(T.p15f[:], T.p15[:], "p15", "p15f")
+    ts(T.p8[:], T.p15f[:], 8.0, None, OP.mult, None, "p15f", "p8")
+    ts(T.EXu[:], T.EXi[:], T.p15f[:], None, OP.add, None, "EXi p15f", "EXu")
+    REM = [(77 * t) % 8 for t in range(NV)]
+    for t in range(NV):
+        ts(T.nc[:, 2 * t:2 * t + 1], T.par[:], float(FW), float(REM[t]), OP.mult, OP.add, "par", "nc%d" % (2 * t))
+        ts(T.nc[:, 2 * t + 1:2 * t + 2], T.par[:], float(-FW), float(FW + REM[t]), OP.mult, OP.add, "par",
+           "nc%d" % (2 * t + 1))
+    for h, nm in ((1, "Ev"), (0, "Od")):
+        cp(T[nm][:], T.D160[:], "D160", nm)
+        for b in range(10):
+            if b % 2 != h:
+                fill(T[nm][:, 16 * b:16 * b + 16], 0.0, nm)
+
+    MAT = {(0, 0): T.Ev[:, 16:144], (0, 1): T.Ev[:, 0:128], (1, 1): T.Od[:, 16:144], (1, 0): T.Od[:, 32:160]}
+
+    def conv(h, l, k, bank):
+        lst = []
+        for gp in range(2):
+            i = 0
+            for part in (h, l):
+                for cc in range(2):
+                    lst.append((T[bank][:, 8 * gp:8 * gp + 8], MAT[(gp, cc)], T[part][:, 16 * k + cc:16 * k + 16:2], i == 0, i == 3))
+                    i += 1
+        return lst
+
+    def arr_s(t, k):
+        act(kk("LA", k), T["land_%d" % k][:, 32 * t:32 * t + 16], ACT.Copy, "land%d_%d" % (t, k), "LA%d" % k, bias=1184.0)
+        act(kk("Lh", k), kk("LA", k), ACT.Copy, "LA%d" % k, "Lh%d" % k)
+
+    def arr_v(t, k):
+        ts(kk("Lu", k), T["land_%d" % k][:, 32 * t:32 * t + 16], float(PAD), None, OP.add, None, "land%d_%d" % (t, k), "Lu%d" % k)
+        tt(kk("Ll", k), kk("LA", k), kk("Lh", k), OP.subtract, "LA%d Lh%d" % (k, k), "Ll%d" % k)
+        mms(conv("Lh", "Ll", k, "MS"), "Lh%d Ll%d Ev Od" % (k, k), "MS")
+        act(kk("LS", k), T.MS[:, 0:16], ACT.Copy, "", "MS LS%d" % k)
+
+    def masks(t, k):
+        IN = T["land_%d" % k][:, 32 * t + 16:32 * t + 32]
+        lk = "land%d_%d" % (t, k)
+        ts(T["n%d" % k][:], IN, 0.0, None, OP.is_lt, None, lk, "n%d" % k)
+        ts(T["u%d" % k][:], IN, float(k - 1), BIG, OP.is_ge, OP.mult, lk, "u%d" % k)
+        if k == 1:
+            tt(T.w1[:], T.n1[:], T.Ep[:], OP.mult, "n1 Ep", "w1")
+        else:
+            ts(T.s20[:], IN, 0.0, None, OP.is_equal, None, lk, "s20")
+            ts(T.s21[:], IN, 1.0, None, OP.is_ge, None, lk, "s21")
+            tt(T.nE[:], T.n2[:], T.Ep[:], OP.mult, "n2 Ep", "nE")
+
+    def npart(t, k, bs, btok):
+        es = btok == "Es"
+        tt(T.z32[:], kk("LS", k), bs, OP.mult, "LS%d" % k + (" Es" if es else ""), "z32" + ("" if es else " CV"))
+        ts(T.nn[:], T.z32[:], 5, 1023, OP.arith_shift_right, OP.bitwise_and, "z32", "nn")
+        for gp in range(2):
+            ts(T.nu[:, gp::2], T.nn[:, 8 * gp:8 * gp + 8], T.nc[:, 2 * t + gp:2 * t + gp + 1], None, OP.add, None,
+               "nn nc%d" % (2 * t + gp), "nu%d" % gp)
+        w0 = 77 * t - REM[t]
+        ts(T.C[:], T.FA[:, w0:2 * FW].indirect(T.nu[:]), float(PAD), None, OP.add, None, "nu0 nu1 FAx0 FAx1 " + FAtok, "C")
+        op("v", lambda e: e.transpose(out=T.CT[:], in_=T.C[:]), "C", "CT")
+        for ch in range(4):
+            cp(T.CTu[:, 64 * ch:64 * ch + 64], T.CT[:, ch::4], "CT", "CTu%d" % ch)
+
+    def xl(k):
+        act(T.XL[:, 256 * k:256 * k + 256], Xw.indirect(kk("Lu", k)), ACT.Copy, "X Xpad Lu%d" % k, "XL%d" % k)
+
+    def qpart(k, off, otok):
+        tt(T.qq[:], Xw.indirect(off), T.XL[:, 256 * k:256 * k + 256], OP.max, "X Xpad %s XL%d" % (otok, k), "qq")
+        for h in range(2):
+            act(T.Q4[:, 512 * h:512 * h + 512], T.qq[:].indirect(T.EXu[:, 32 * h:32 * h + 32]), ACT.Copy, "qq EXu", "Q4%d" % h)
+
+    def starts(ch):
+        d = T["D%d" % ch][:, 0:64]
+        return [(d, T.I32[:], T.CT[:, ch::4], True, False),
+                (d, T.oneb[0:1, :], T.MK[0:1, 64 * ch:64 * ch + 64], False, False)]
+
+    def sums(ch, ps, last):
+        return [(T["D%d" % ch][:, 0:64], T.W65[:, 15 - p:143 - p], T["z%d" % ch][:, p::16], False, last and p == ps[-1])
+                for p in ps]
+
+    def fused(ch, h, w):
+        a, b, q = (0, 64, "Q40 Q41") if h is None else (32 * h, 32 * h + 32, "Q4%d" % h)
+        tt(T["z%d" % ch][:, 16 * a:16 * b], Xw.indirect(T.CTu[:, 64 * ch + a:64 * ch + b]),
+           T.Q4[:, 16 * a:16 * b], OP.subtract, "X Xpad CTu%d %s" % (ch, q), w)
+
+    def absz(a, tok):
+        act(a, a, ACT.Abs, tok, tok)
+
+    ALL = list(range(16))
+
+    def main(k):
+        act(T.z3[:], Xw.indirect(T.CTu[:, 192:256]), ACT.Copy, "X Xpad CTu3", "z3")
+        for ch in range(4):
+            mms(starts(ch), "CT I32 oneb MK", "D%d" % ch)
+        for h in range(2):
+            mms([(T.q4ps[:, 512 * h:512 * h + 512], T.IB[:], T.Q4[:, 512 * h:512 * h + 512], True, True)], "IB Q4%d" % h, "qp%d" % h)
+        fused(0, 0, "z0a")
+        fused(0, 1, "z0b")
+        absz(T.z0[:], "z0a z0b")
+        mms(sums(0, ALL, True), "z0a z0b W65", "D0")
+        fused(1, None, "z1")
+        absz(T.z1[:], "z1")
+        mms(sums(1, ALL, True), "z1 W65", "D1")
+        tt(T.z3[:], T.z3[:], T.q4ps[:], OP.subtract, "z3", "z3 qp0 qp1")
+        absz(T.z3[:], "z3")
+        mms(sums(3, ALL, True), "z3 W65", "D3")
+        fused(2, 0, "z2a")
+        absz(T.z2[:, 0:512], "z2a")
+        fused(2, 1, "z2e z2o")
+        absz(T.z2[:, 512::2], "z2e")
+        mms(sums(2, ALL[0::2], False), "z2a z2e W65", "D2")
+        absz(T.z2[:, 513::2], "z2o")
+        mms(sums(2, ALL[1::2], True), "z2a z2o W65", "D2")
+
+    def scan(ch):
+        op("v", lambda e: e.tensor_tensor_scan(out=T["SC%d" % ch][:], data0=T.RST[:], data1=T["D%d" % ch][:, 0:64],
+                                               initial=BIG, op0=OP.max, op1=OP.min), "RST", "SC%d D%d" % (ch, ch))
+
+    def scans01():
+        scan(0)
+        scan(1)
+        tt(T.M[:], T.SC0[:, 3::4], T.SC1[:, 3::4], OP.min, "SC0 SC1", "M")
+
+    def scans32(k):
+        scan(3)
+        tt(T.M[:], T.M[:], T.SC3[:, 3::4], OP.min, "M SC3", "M")
+        if k < NR - 1:
+            tt(T.Mu[:], T.M[:], T["u%d" % (k + 1)][:], OP.min, "M u%d" % (k + 1), "Mu")
+        scan(2)
+
+    def chain(k):
+        tt(T.t1[:], T.Mu[:], T.SC2[:, 3::4], OP.min, "Mu SC2", "t1")
+        tt(T.t2[:], T.t1[:], T["w%d" % k][:], OP.max, "t1 w%d" % k, "t2")
+        ts(T.bi[:], T.t2[:], 4095, None, OP.bitwise_and, None, "t2", "bi")
+        cp(T.bh[:], T.bi[:], "bi", "bh")
+        tt(T.bl[:], T.bi[:], T.bh[:], OP.subtract, "bi bh", "bl")
+        mms(conv("bh", "bl", 0, "CV"), "bh bl Ev Od", "CV")
+        cp(T.bu[:], T.bi[:], "bi", "bu")
+        qpart(k, T.bu[:], "bu")
+
+    def keys(k):
+        tt(kk("K", k), T.M[:], T.SC2[:, 3::4], OP.min, "M SC2", "K%d" % k)
+        ts(kk("B", k), kk("K", k), 4095, None, OP.bitwise_and, None, "K%d" % k, "B%d" % k)
+        tc = T.Tk[:, k:k + 1]
+        if k == 0:
+            ts(kk("lv", 0), kk("K", 0), tc, None, OP.is_lt, None, "K0 Tk", "lv0")
+        else:
+            ts(T.lt[:], kk("K", k), tc, None, OP.is_lt, None, "K%d Tk" % k, "lt")
+            tt(kk("lv", k), T.lt[:], T["g%d" % k][:], OP.mult, "lt g%d" % k, "lv%d" % k)
+        tt(T.yo[:], kk("B", k), kk("lv", k), OP.mult, "B%d lv%d" % (k, k), "yo")
+        cp(kk("yu", k), T.yo[:], "yo", "yu%d" % k)
+
+    def rewire_pre(t, k):
+        P, ptok = (T.Er, "Er") if k == 0 else (T["P%dr" % k], "P%dr" % k)
+        if k == 1:
+            tt(T.px[:], kk("B", 0), T.Ep[:], OP.subtract, "B0 Ep", "px")
+            tt(T.px[:], T.px[:], kk("lv", 0), OP.mult, "px lv0", "px")
+            tt(T.P1p[:], T.px[:], T.Ep[:], OP.add, "px Ep", "P1p")
+            tt(T.P1r[:], T.px[:], T.Er[:], OP.add, "px Er", "P1r")
+        if k == 2:
+            tt(T.px[:], kk("B", 1), T.P1p[:], OP.subtract, "B1 P1p", "px")
+            tt(T.px[:], T.px[:], kk("lv", 1), OP.mult, "px lv1", "px")
+            tt(T.P2r[:], T.px[:], T.P1r[:], OP.add, "px P1r", "P2r")
+        tt(T.rz[:], kk("LA", k), P[:], OP.mult, "LA%d %s" % (k, ptok), "rz")
+        z, ztok = T.rz, "rz"
+        if k:
+            ts(T.rz2[:], T.rz[:], 32.0 * k, None, OP.add, None, "rz", "rz2")
+            z, ztok = T.rz2, "rz2"
+        ts(T.NW[:, 0:16], z[:], 5, 2047, OP.arith_shift_right, OP.bitwise_and, ztok, "NW0")
+        if k == 1:
+            ts(T.NW[:, 16:32], kk("lv", 0), -1.0, None, OP.add, None, "lv0", "NW1")
+        if k == 2:
+            ts(T.p2[:], kk("lv", 1), 2.0, -1.0, OP.mult, OP.add, "lv1", "p2")
+            ts(T.ga[:], kk("lv", 0), -1.0, None, OP.add, None, "lv0", "ga")
+            tt(T.NW[:, 16:32], T.p2[:], T.ga[:], OP.max, "p2 ga", "NW1")
+        n = 32 if k else 16
+        tt(T.df[:, 0:n], T.NW[:, 0:n], T["land_%d" % k][:, 32 * t:32 * t + n], OP.subtract,
+           "NW0 land%d_%d" % (t, k) + (" NW1" if k else ""), "df")
+
+    def rewire(t, k):
+        n = 32 if k else 16
+        for h in range(n // 16):
+            act(T.dd[:, 16 * h:16 * h + 16], kk("lv", k), ACT.Copy, "lv%d" % k, "dd%d" % h, bias=1.0, scale=-1.0)
+        tt(T.df[:, 0:n], T.df[:, 0:n], T.dd[:, 0:n], OP.mult, "df dd0" + (" dd1" if k else ""), "df")
+        src = T["src_%d" % k][:, 32 * t:32 * t + n]
+        tt(src, T.df[:, 0:n], T["land_%d" % k][:, 32 * t:32 * t + n], OP.add, "df land%d_%d" % (t, k), "src%d_%d" % (t, k))
+        dst = T.cores[(rank + 1) % n_ranks if t < NV - 1 else (rank - t) % n_ranks]
+        before("g", ["src%d_%d" % (t, k)], [])
+        rid, pid = topo.addr(dst, core)
+        ar = "ar%d_%d" % (t + 1, k)
+        g.remote_dma(T["land_%d" % k][:, 32 * (t + 1):32 * (t + 1) + n], src, T.sem[ar], T.sem.ls, pid, rid, topo.mask(core, dst))
+        ne = len(topo.engines(core, dst))
+        sent[0] += ne
+        lastw["land%d_%d" % (t + 1, k)] = (ar, ne, "remote")
+
+    def thresholds():
+        mms([(T.CV[:, 0:48], T.oneb[:], T.lv[:], True, True)], "oneb lv0 lv1 lv2", "CV")
+        op("v", lambda e: e.tensor_reduce(out=T.cnt[:], in_=T.CV[:, 0:48], axis=AxisListType.X, op=OP.add), "", "cnt CV")
+        ts(T.ai[:], T.cnt[:], -1.0, 6144.0, OP.mult, OP.add, "cnt", "ai")
+        ts(T.ai2[:], T.ai[:], 31, None, OP.bitwise_and, None, "ai", "ai2")
+        ts(T.af[:], T.ai2[:], 65536.0, None, OP.mult, None, "ai2", "af")
+        ts(T.Tk[:], T.thk[:], T.af[:], None, OP.add, None, "thk af", "Tk")
+
+    ts(T.Ep[:], T.exi[:], float(PAD), None, OP.add, None, "exi", "Ep")
+    cp(T.eh[:], T.Ep[:], "Ep", "eh")
+    tt(T.el[:], T.Ep[:], T.eh[:], OP.subtract, "Ep eh", "el")
+    mms(conv("eh", "el", 0, "CV"), "eh el Ev Od", "CV")
+    act(T.Es[:], T.CV[:, 0:16], ACT.Copy, "", "CV Es")
+    cp(T.land_0[:, 0:16], T.lci[:, 0:16], "lci", "land0_0")
+    arr_s(0, 0)
+    arr_v(0, 0)
+    cp(T.Er[:], T.exi[:], "exi", "Er")
+    cp(T.Eu[:], T.Ep[:], "Ep", "Eu")
+    ts(T.W65[:], T.W[:], 65536.0, None, OP.mult, None, "W", "W65")
+    cp(T.IB[:], T.I32[:], "I32", "IB")
+    ts(T.RST[:], T.RST[:], BIG, None, OP.mult, None, "RST", "RST")
+    npart(0, 0, T.Es[:], "Es")
+    xl(0)
+
+    for t in range(NV):
+        qpart(0, T.Eu[:], "Eu")
+        if t == 0:
+            for b in range(2):
+                dma("y", T.FA[:, b * FW + 1024:(b + 1) * FW], T.FA[:, b * FW:b * FW + FW - 1024], "dfw", 32, FAtok, "FAx%d" % b)
+            for k in (1, 2):
+                cp(T["land_%d" % k][:, 0:16], T.lci[:, 16 * k:16 * k + 16], "lci", "land0_%d" % k)
+                cp(T["land_%d" % k][:, 16:32], T.upi[:, 16 * k:16 * k + 16], "upi", "land0_%d" % k)
+            cp(T.thf[:], T.thi[:], "thi", "thf")
+            ts(T.tsel[:], T.tsel[:], 65536.0, None, OP.mult, None, "tsel", "tsel")
+            mms([(T.MS[:, 0:3], T.tsel[:], T.thf[:], True, True)], "tsel thf", "MS")
+            act(T.thk[:], T.MS[:, 0:3], ACT.Copy, "", "MS thk")
+            act(T.Tk[:], T.thk[:], ACT.Copy, "thk", "Tk")
+            cp(T.wtf[:], T.wti[:], "wti", "wtf")
+            ts(T.SW[:], T.W[:], T.wtf[:], None, OP.mult, None, "W wtf", "SW")
+            ts(T.base[:], T.b128[:], T.p8[:], None, OP.add, None, "b128 p8", "base")
+            fill(T.mone[:], -1.0, "mone")
+            dma("y", T.yi[:, 0:16], T.mone[:], "dout", 96, "mone", "yi0")
+        else:
+            rewire_pre(t - 1, 1)
+            rewire(t - 1, 1)
+            rewire_pre(t - 1, 2)
+            rewire(t - 1, 2)
+            thresholds()
+        main(0)
+        arr_s(t, 1)
+        arr_v(t, 1)
+        masks(t, 1)
+        xl(1)
+        scans01()
+        rewire_pre(t, 0)
+        scans32(0)
+        chain(1)
+        npart(t, 1, T.CV[:, 0:16], "CV")
+        main(1)
+        keys(0)
+        act(T.y0[:], Xw.indirect(kk("yu", 0)), ACT.Copy, "X Xpad yu0", "y0")
+        rewire(t, 0)
+        arr_s(t, 2)
+        arr_v(t, 2)
+        xl(2)
+        masks(t, 2)
+        tt(T.sB[:], T.s20[:], kk("B", 0), OP.mult, "s20 B0", "sB")
+        tt(T.w2[:], T.sB[:], T.nE[:], OP.add, "sB nE", "w2")
+        scans01()
+        tt(T.g1[:], T.n1[:], kk("lv", 0), OP.max, "n1 lv0", "g1")
+        scans32(1)
+        chain(2)
+        npart(t, 2, T.CV[:, 0:16], "CV")
+        main(2)
+        keys(1)
+        tt(T.y01[:], Xw.indirect(kk("yu", 1)), T.y0[:], OP.max, "X Xpad yu1 y0", "y01")
+        if t < NV - 1:
+            arr_s(t + 1, 0)
+            arr_v(t + 1, 0)
+        tt(T.ga[:], T.s20[:], kk("lv", 0), OP.mult, "s20 lv0", "ga")
+        tt(T.gb[:], T.s21[:], kk("lv", 1), OP.mult, "s21 lv1", "gb")
+        tt(T.ga[:], T.ga[:], T.gb[:], OP.max, "ga gb", "ga")
+        tt(T.g2[:], T.ga[:], T.n2[:], OP.max, "ga n2", "g2")
+        scans01()
+        scans32(2)
+        keys(2)
+        tt(T.yy[:], Xw.indirect(kk("yu", 2)), T.y01[:], OP.max, "X Xpad yu2 y01", "yy")
+        mms([(T.CV[:, 0:16], T.SW[:, 15 - p:143 - p], T.yy[:, p::16], p == 0, p == 15) for p in ALL], "SW yy", "CV")
+        if t < NV - 1:
+            npart(t + 1, 0, T.Es[:], "Es")
+        else:
+            rewire_pre(t, 1)
+            rewire(t, 1)
+            rewire_pre(t, 2)
+            rewire(t, 2)
+        cp(T.si[:], T.CV[:, 0:16], "", "si CV")
+        ts(T.sm[:], T.si[:], 7, None, OP.bitwise_and, None, "si", "sm")
+        tt(T.sa[:], T.sm[:], T.base[:], OP.add, "sm base", "sa")
+        cp(T.wu[:], T.sa[:], "sa", "wu")
+        op("v", lambda e: e.tensor_copy(out=Xw.indirect(T.wu[:]), in_=T.yy[:]), "wu yy", "X Xpad")
+        if t < NV - 1:
+            xl(0)
+
+    dma("s", T.yx[:], T.X[:, PAD:PAD + 2048], "dx", 32, "X Xpad", "yxo")
+    for k in range(NR):
+        tok = "land%d_%d" % (NV, k)
+        dma("y", T.yl[:, 16 * k:16 * k + 16], T["land_%d" % k][:, 32 * NV:32 * NV + 16], "dout", 96, tok, "ylo%d" % k)
+        if k:
+            dma("y", T.yi[:, 16 * k:16 * k + 16], T["land_%d" % k][:, 32 * NV + 16:32 * NV + 32], "dout", 96, tok, "yio%d" % k)
+    need("g", "dout", 96)
+    need("g", "dx", 32)
+    need("g", "ls", sent[0])
+    for q in ("v", "s", "p", "g"):
+        need("g", "c" + q, count[q])

@@ -16,46 +16,51 @@ def _decl(where, dtype, names, n, rows=128):
 
 _decl("sbuf", "bfloat16", "X", 2080)
 _decl("sbuf", "int32", "FA", 2 * FW)
-_decl("sbuf", "float32", "C CT", 256)
+_decl("sbuf", "float32", "C CT SA RSA onef", 256)
 _decl("sbuf", "uint16", "CTu", 256)
 _decl("sbuf", "bfloat16", "qq yy y0 y01", 256)
 _decl("sbuf", "bfloat16", "Q4 z0 z1 z2 z3", 1024)
 _decl("psum", "float32", "q4ps", 1024)
-_decl("psum", "float32", "CV MS D0 D1 D2 D3", 512)
-_decl("sbuf", "float32", "SC0 SC1 SC2 SC3 RST", 64)
-_decl("sbuf", "int32", "EXi", 64)
-_decl("sbuf", "uint16", "EXu", 64)
+_decl("psum", "float32", "CV MS DA DB", 512)
+_decl("sbuf", "float32", "SB RSB", 64)
+_decl("sbuf", "int32", "EXi", 32)
+_decl("sbuf", "uint16", "EXu", 32)
 _decl("sbuf", "int32", "lci upi", 48)
 _decl("sbuf", "int32", "thi", 3, 8)
 _decl("sbuf", "float32", "thf", 3, 8)
 _decl("sbuf", "float32", "tsel", 128, 8)
 _decl("sbuf", "bfloat16", "MK", 256, 1)
+_decl("sbuf", "bfloat16", "MK2", 64, 1)
 _decl("sbuf", "int32", "wti ai ai2 pi pg p15", 1)
 _decl("sbuf", "float32", "wtf cnt af par p8 p15f", 1)
 _decl("sbuf", "float32", "thk Tk", 3)
 _decl("sbuf", "float32", "nc", 8)
-_decl("sbuf", "float32", "onef D160", 160)
+_decl("sbuf", "float32", "D160", 160)
 _decl("sbuf", "bfloat16", "Ev Od", 160)
 _decl("sbuf", "float32", "W", 144)
 _decl("sbuf", "bfloat16", "W65 SW", 144)
 _decl("sbuf", "float32", "I32", 128)
 _decl("sbuf", "bfloat16", "IB oneb", 128)
-_decl("sbuf", "int32", "exi b128 base z32 nn t2 bi rz rz2 si sm sa", 16)
+_decl("sbuf", "int32", "exi b128 base z32 nn t2 bi rz0 NW0 si sm sa", 16)
 _decl("sbuf", "uint16", "Eu nu bu wu", 16)
 _decl("sbuf", "bfloat16", "eh el bh bl lt", 16)
-_decl("sbuf", "float32", "mone Ep Er Es M Mu t1 yo n1 u1 w1 n2 u2 w2 s20 s21 nE sB g1 g2 ga gb px P1p P1r P2r p2", 16)
-_decl("sbuf", "int32", "NW", 32)
-_decl("sbuf", "float32", "df dd", 32)
+_decl("sbuf", "float32", "mone Ep Er Es Mu t1 yo u1 w1 u2 w2 s20 s21 nE sB g1 g2 ga gb px qx df0 x0 a2 pa pb", 16)
+_decl("sbuf", "float32", "n12 P12 LAk rz12", 32)
+_decl("sbuf", "int32", "rk12", 32)
+_decl("sbuf", "int32", "NW", 64)
+_decl("sbuf", "float32", "df xx lvd", 64)
 _decl("sbuf", "bfloat16", "lv Lh Ll", 48)
 _decl("sbuf", "uint16", "Lu yu", 48)
 _decl("sbuf", "float32", "LA LS", 48)
 _decl("sbuf", "int32", "K B", 48)
 _decl("sbuf", "bfloat16", "XL", 768)
-_decl("sbuf", "float32", "land_0 land_1 land_2", 160)
-_decl("sbuf", "float32", "src_0 src_1 src_2", 128)
+_decl("sbuf", "float32", "land0", 5 * 16)
+_decl("sbuf", "float32", "land1", 5 * 64)
+_decl("sbuf", "float32", "src0", 4 * 16)
+_decl("sbuf", "float32", "src1", 4 * 64)
 
-SEMAPHORES = ["cv", "cs", "cp", "cg", "ls", "dfa", "dfw", "dx", "dlc", "dup", "dex", "dth", "dwt", "dout"]
-SEMAPHORES += ["ar%d_%d" % (t, k) for t in range(1, 5) for k in range(NR)]
+SEMAPHORES = ["cv", "cs", "cp", "cg", "ls", "dfa", "dfw", "dx", "dy", "dlc", "dup", "dex", "dth", "dwt", "dout"]
+SEMAPHORES += ["ar%d_%d" % (t, k) for t in range(1, 5) for k in range(2)]
 
 
 def rank_program(g, core, T, topo):
@@ -147,15 +152,22 @@ def rank_program(g, core, T, topo):
     def kk(nm, k):
         return T[nm][:, 16 * k:16 * k + 16]
 
+    def weave(a, b):
+        for i in range(max(len(a), len(b))):
+            for l in (a, b):
+                if i < len(l) and l[i]:
+                    l[i]()
+
     Xw = T.X[:, 0:2080]
 
     dma("y", T.exi[:], T.ex[:], "dex", 16, "", "exi")
     dma("s", T.lci[:], T.lc[:], "dlc", 16, "", "lci")
+    dma("y", T.X[:, PAD:PAD + 2048], T.xs[:], "dx", 16, "", "X")
     it = [0]
 
     def lfa(rows, src, blk):
         for (a, b, c) in ((0, ROT, 1024), (1024 - ROT, 0, ROT)):
-            q = "ys"[it[0] % 2]
+            q = "sy"[it[0] % 2]
             it[0] += 1
             dma(q, T.FA[rows, blk * FW + a:blk * FW + a + c - b], T.fa[src, b:c], "dfa", 288, "", "FA%d" % it[0])
     lfa(slice(0, 128), slice(0, 128), 0)
@@ -163,25 +175,28 @@ def rank_program(g, core, T, topo):
         o = G ^ 1
         lfa(slice(16 * G, 16 * G + 16), slice(16 * o, 16 * o + 16), 1)
     FAtok = " ".join("FA%d" % (i + 1) for i in range(it[0]))
-    dma("y", T.X[:, PAD:PAD + 2048], T.xs[:], "dx", 16, "", "X")
-    dma("s", T.upi[:], T.up[:], "dup", 16, "", "upi")
-    dma("s", T.thi[:], T.th[:], "dth", 16, "", "thi")
-    dma("s", T.wti[:], T.wt[:], "dwt", 16, "", "wti")
+    dma("y", T.upi[:], T.up[:], "dup", 16, "", "upi")
+    dma("y", T.thi[:], T.th[:], "dth", 16, "", "thi")
+    dma("y", T.wti[:], T.wt[:], "dwt", 16, "", "wti")
 
     fill(T.onef[:], 1.0, "onef")
     op("g", lambda e: e.iota(T.pi[:], [[0, 1]], 0, 1), "", "pi")
 
     def aff(o, a, pat, f, base, cm, r, w):
         op("g", lambda e: e.affine_select(o, a, pat, f, 0.0, base, cm), r, w)
-    aff(T.D160[:], T.onef[:], [[-1, 160]], OP.is_equal, 16, 1, "onef", "D160")
-    op("g", lambda e: e.iota(T.EXi[:], [[16, 16], [0, 4]], 0, 0), "", "EXi")
+
+    def iob(o, pat, base, w):
+        op("g", lambda e: e.iota(o, pat, base, 0, allow_small_or_imprecise_dtypes=True), "", w)
+    aff(T.D160[:], T.onef[:, 0:160], [[-1, 160]], OP.is_equal, 16, 1, "onef", "D160")
+    op("g", lambda e: e.iota(T.EXi[:], [[16, 8], [0, 4]], 0, 0), "", "EXi")
     aff(T.I32[:], T.onef[:, 0:128], [[-1, 128]], OP.is_equal, 0, 1, "onef", "I32")
-    op("g", lambda e: e.iota(T.MK[0:1, :], [[4096, 4], [0, 16], [16384, 4]], 0, 0,
-                             allow_small_or_imprecise_dtypes=True), "", "MK")
+    iob(T.MK[0:1, :], [[0, 16], [4096, 16]], 0, "MK")
+    iob(T.MK2[0:1, :], [[0, 16], [16384, 4]], 8192, "MK2")
     aff(T.W[:], T.onef[:, 0:144], [[-16, 9], [0, 16]], OP.is_ge, 0, 1, "onef", "W")
     aff(T.W[:], T.W[:], [[16, 9], [0, 16]], OP.is_ge, 15, -1, "W", "W")
     aff(T.W[:], T.W[:], [[0, 9], [1, 16]], OP.is_equal, -15, 0, "W", "W")
-    aff(T.RST[:], T.onef[:, 0:64], [[0, 16], [1, 4]], OP.is_equal, 0, 0, "onef", "RST")
+    aff(T.RSA[:], T.onef[:], [[0, 16], [1, 16]], OP.is_equal, 0, 0, "onef", "RSA")
+    aff(T.RSB[:], T.onef[:, 0:64], [[0, 16], [1, 4]], OP.is_equal, 0, 0, "onef", "RSB")
     op("g", lambda e: e.iota(T.b128[:], [[128, 16]], PAD, 0), "", "b128")
     aff(T.tsel[:], T.onef[0:8, 0:128], [[1, 128]], OP.is_ge, 0, -16, "onef", "tsel")
     aff(T.tsel[:], T.tsel[:], [[-1, 128]], OP.is_ge, 15, 16, "tsel", "tsel")
@@ -209,67 +224,100 @@ def rank_program(g, core, T, topo):
 
     MAT = {(0, 0): T.Ev[:, 16:144], (0, 1): T.Ev[:, 0:128], (1, 1): T.Od[:, 16:144], (1, 0): T.Od[:, 32:160]}
 
-    def conv(h, l, k, bank):
-        lst = []
+    def conv(h, l, bank, a=0, e=16):
+        lst, n = [], (e - a) // 2
         for gp in range(2):
             i = 0
             for part in (h, l):
                 for cc in range(2):
-                    lst.append((T[bank][:, 8 * gp:8 * gp + 8], MAT[(gp, cc)], T[part][:, 16 * k + cc:16 * k + 16:2], i == 0, i == 3))
+                    lst.append((T[bank][:, n * gp:n * gp + n], MAT[(gp, cc)], T[part][:, a + cc:e:2], i == 0, i == 3))
                     i += 1
         return lst
 
-    def arr_s(t, k):
-        act(kk("LA", k), T["land_%d" % k][:, 32 * t:32 * t + 16], ACT.Copy, "land%d_%d" % (t, k), "LA%d" % k, bias=1184.0)
-        act(kk("Lh", k), kk("LA", k), ACT.Copy, "LA%d" % k, "Lh%d" % k)
+    def codes(t, w):
+        return T.land1[:, 64 * t:64 * t + 32] if w else T.land0[:, 16 * t:16 * t + 16]
 
-    def arr_v(t, k):
-        ts(kk("Lu", k), T["land_%d" % k][:, 32 * t:32 * t + 16], float(PAD), None, OP.add, None, "land%d_%d" % (t, k), "Lu%d" % k)
-        tt(kk("Ll", k), kk("LA", k), kk("Lh", k), OP.subtract, "LA%d Lh%d" % (k, k), "Ll%d" % k)
-        mms(conv("Lh", "Ll", k, "MS"), "Lh%d Ll%d Ev Od" % (k, k), "MS")
-        act(kk("LS", k), T.MS[:, 0:16], ACT.Copy, "", "MS LS%d" % k)
+    COL = (slice(0, 16), slice(16, 48))
 
-    def masks(t, k):
-        IN = T["land_%d" % k][:, 32 * t + 16:32 * t + 32]
-        lk = "land%d_%d" % (t, k)
-        ts(T["n%d" % k][:], IN, 0.0, None, OP.is_lt, None, lk, "n%d" % k)
-        ts(T["u%d" % k][:], IN, float(k - 1), BIG, OP.is_ge, OP.mult, lk, "u%d" % k)
-        if k == 1:
-            tt(T.w1[:], T.n1[:], T.Ep[:], OP.mult, "n1 Ep", "w1")
-        else:
-            ts(T.s20[:], IN, 0.0, None, OP.is_equal, None, lk, "s20")
-            ts(T.s21[:], IN, 1.0, None, OP.is_ge, None, lk, "s21")
-            tt(T.nE[:], T.n2[:], T.Ep[:], OP.mult, "n2 Ep", "nE")
+    def arr_s(t, w):
+        act(T.LA[:, COL[w]], codes(t, w), ACT.Copy, "land%d_%d" % (t, w), "LA%d" % w, bias=1184.0)
+        act(T.Lh[:, COL[w]], T.LA[:, COL[w]], ACT.Copy, "LA%d" % w, "Lh%d" % w)
+
+    def arr_u(t, w):
+        ts(T.Lu[:, COL[w]], codes(t, w), float(PAD), None, OP.add, None, "land%d_%d" % (t, w), "Lu%d" % w)
+
+    def arr_l(w):
+        tt(T.Ll[:, COL[w]], T.LA[:, COL[w]], T.Lh[:, COL[w]], OP.subtract, "LA%d Lh%d" % (w, w), "Ll%d" % w)
+        mms(conv("Lh", "Ll", "MS", 16, 48) if w else conv("Lh", "Ll", "MS"), "Lh%d Ll%d Ev Od" % (w, w), "MS")
+
+    def arr_e(w):
+        if not w:
+            act(T.LS[:, 0:16], T.MS[:, 0:16], ACT.Copy, "", "MS LS0")
+        for k in (1, 2) if w else ():
+            for gp in range(2):
+                act(T.LS[:, 16 * k + 8 * gp:16 * k + 8 * gp + 8], T.MS[:, 16 * gp + 8 * k - 8:16 * gp + 8 * k], ACT.Copy,
+                    "", "MS LS%d" % k)
+
+    def masks1(t):
+        act(T.n12[:], T.land1[:, 64 * t + 32:64 * t + 64], ACT.Relu, "land%d_1" % t, "n12", scale=-1.0)
+        act(T.u1[:], T.n12[:, 0:16], ACT.Copy, "n12", "u1", scale=-BIG, bias=BIG)
+
+    def masks2(t):
+        IN, lk = T.land1[:, 64 * t + 48:64 * t + 64], "land%d_1" % t
+        act(T.s21[:], IN, ACT.Relu, lk, "s21")
+        act(T.u2[:], T.s21[:], ACT.Copy, "s21", "u2", scale=BIG)
+        act(T.a2[:], IN, ACT.Abs, lk, "a2")
+        act(T.s20[:], T.a2[:], ACT.Copy, "a2", "s20", scale=-1.0, bias=1.0)
+        for k in (1, 2):
+            act(T.LAk[:, 16 * k - 16:16 * k], kk("LA", k), ACT.Copy, "LA1", "LAk%d" % k, scale=-32.0, bias=32.0 * k)
 
     def npart(t, k, bs, btok):
         es = btok == "Es"
-        tt(T.z32[:], kk("LS", k), bs, OP.mult, "LS%d" % k + (" Es" if es else ""), "z32" + ("" if es else " CV"))
-        ts(T.nn[:], T.z32[:], 5, 1023, OP.arith_shift_right, OP.bitwise_and, "z32", "nn")
-        for gp in range(2):
-            ts(T.nu[:, gp::2], T.nn[:, 8 * gp:8 * gp + 8], T.nc[:, 2 * t + gp:2 * t + gp + 1], None, OP.add, None,
-               "nn nc%d" % (2 * t + gp), "nu%d" % gp)
         w0 = 77 * t - REM[t]
-        ts(T.C[:], T.FA[:, w0:2 * FW].indirect(T.nu[:]), float(PAD), None, OP.add, None, "nu0 nu1 FAx0 FAx1 " + FAtok, "C")
-        op("v", lambda e: e.transpose(out=T.CT[:], in_=T.C[:]), "C", "CT")
-        for ch in range(4):
-            cp(T.CTu[:, 64 * ch:64 * ch + 64], T.CT[:, ch::4], "CT", "CTu%d" % ch)
 
-    def xl(k):
-        act(T.XL[:, 256 * k:256 * k + 256], Xw.indirect(kk("Lu", k)), ACT.Copy, "X Xpad Lu%d" % k, "XL%d" % k)
+        def nu(gp):
+            return lambda: ts(T.nu[:, gp::2], T.nn[:, 8 * gp:8 * gp + 8], T.nc[:, 2 * t + gp:2 * t + gp + 1], None, OP.add,
+                              None, "nn nc%d" % (2 * t + gp), "nu%d" % gp)
 
-    def qpart(k, off, otok):
-        tt(T.qq[:], Xw.indirect(off), T.XL[:, 256 * k:256 * k + 256], OP.max, "X Xpad %s XL%d" % (otok, k), "qq")
+        def ctu(ch):
+            return lambda: cp(T.CTu[:, 64 * ch:64 * ch + 64], T.CT[:, ch::4], "CT", "CTu%d" % ch)
+        return [
+            lambda: tt(T.z32[:], kk("LS", k), bs, OP.mult, "LS%d" % k + (" Es" if es else ""), "z32" + ("" if es else " CV")),
+            lambda: ts(T.nn[:], T.z32[:], 5, 1023, OP.arith_shift_right, OP.bitwise_and, "z32", "nn"),
+            nu(0), nu(1),
+            lambda: ts(T.C[:], T.FA[:, w0:2 * FW].indirect(T.nu[:]), float(PAD), None, OP.add, None,
+                       "nu0 nu1 FAx0 FAx1 " + FAtok, "C"),
+            lambda: op("v", lambda e: e.transpose(out=T.CT[:], in_=T.C[:]), "C", "CT"),
+            ctu(3), ctu(0), ctu(1), ctu(2)]
+
+    def xl(k, halves=(slice(0, 16),)):
+        for s in halves:
+            act(T.XL[:, 256 * k + 16 * s.start:256 * k + 16 * s.stop], Xw.indirect(T.Lu[:, 16 * k + s.start:16 * k + s.stop]),
+                ACT.Copy, "X Xpad Lu%d" % min(k, 1), "XL%d_%d" % (k, s.start))
+
+    HALVES = (slice(0, 8), slice(8, 16))
+
+    def qpart(k, off, otok, halves=(slice(0, 16),)):
+        for s in halves:
+            a, e = 16 * s.start, 16 * s.stop
+            tt(T.qq[:, a:e], Xw.indirect(off[:, s]), T.XL[:, 256 * k + a:256 * k + e], OP.max,
+               "X Xpad %s XL%d_%d" % (otok, k, s.start), "qq1" if a else ("qq0" if e < 256 else "qq0 qq1"))
         for h in range(2):
-            act(T.Q4[:, 512 * h:512 * h + 512], T.qq[:].indirect(T.EXu[:, 32 * h:32 * h + 32]), ACT.Copy, "qq EXu", "Q4%d" % h)
+            act(T.Q4[:, 512 * h:512 * h + 512], T.qq[:, 128 * h:128 * h + 128].indirect(T.EXu[:]), ACT.Copy,
+                "qq%d EXu" % h, "Q4%d" % h)
 
-    def starts(ch):
-        d = T["D%d" % ch][:, 0:64]
-        return [(d, T.I32[:], T.CT[:, ch::4], True, False),
-                (d, T.oneb[0:1, :], T.MK[0:1, 64 * ch:64 * ch + 64], False, False)]
+    PLACE = {ch: ("DA", T.DA[:, ch:256:4]) for ch in (0, 1, 3)}
+    PLACE[2] = ("DB", T.DB[:, 0:64])
 
-    def sums(ch, ps, last):
-        return [(T["D%d" % ch][:, 0:64], T.W65[:, 15 - p:143 - p], T["z%d" % ch][:, p::16], False, last and p == ps[-1])
-                for p in ps]
+    def starts():
+        mms([(T.DA[:, 0:256], T.I32[:], T.CT[:], True, False),
+             (T.DA[:, 0:256], T.oneb[0:1, :], T.MK[0:1, :], False, False)], "CT I32 oneb MK", "DA")
+        mms([(T.DB[:, 0:64], T.I32[:], T.CT[:, 2::4], True, False),
+             (T.DB[:, 0:64], T.oneb[0:1, :], T.MK2[0:1, :], False, False)], "CT I32 oneb MK2", "DB")
+
+    def sums(ch, ps, last, r):
+        tok, d = PLACE[ch]
+        mms([(d, T.W65[:, 15 - p:143 - p], T["z%d" % ch][:, p::16], False, last and p == ps[-1]) for p in ps], r + " W65", tok)
 
     def fused(ch, h, w):
         a, b, q = (0, 64, "Q40 Q41") if h is None else (32 * h, 32 * h + 32, "Q4%d" % h)
@@ -281,222 +329,236 @@ def rank_program(g, core, T, topo):
 
     ALL = list(range(16))
 
-    def main(k):
-        act(T.z3[:], Xw.indirect(T.CTu[:, 192:256]), ACT.Copy, "X Xpad CTu3", "z3")
-        for ch in range(4):
-            mms(starts(ch), "CT I32 oneb MK", "D%d" % ch)
+    def pair(ch, toks):
+        z = T["z%d" % ch]
+        for s in range(2):
+            absz(z[:, s::2], toks[s])
+            sums(ch, ALL[s::2], s == 1 and ch == 1, toks[s])
+
+    def main():
+        for h in range(2):
+            act(T.z3[:, 512 * h:512 * h + 512], Xw.indirect(T.CTu[:, 192 + 32 * h:224 + 32 * h]), ACT.Copy,
+                "X Xpad CTu3", "z3e%d z3o%d" % (h, h))
+        starts()
         for h in range(2):
             mms([(T.q4ps[:, 512 * h:512 * h + 512], T.IB[:], T.Q4[:, 512 * h:512 * h + 512], True, True)], "IB Q4%d" % h, "qp%d" % h)
-        fused(0, 0, "z0a")
-        fused(0, 1, "z0b")
-        absz(T.z0[:], "z0a z0b")
-        mms(sums(0, ALL, True), "z0a z0b W65", "D0")
-        fused(1, None, "z1")
-        absz(T.z1[:], "z1")
-        mms(sums(1, ALL, True), "z1 W65", "D1")
-        tt(T.z3[:], T.z3[:], T.q4ps[:], OP.subtract, "z3", "z3 qp0 qp1")
-        absz(T.z3[:], "z3")
-        mms(sums(3, ALL, True), "z3 W65", "D3")
+        fused(0, 0, "z0e z0o")
+        fused(0, 1, "z0e z0o")
+        pair(0, ("z0e", "z0o"))
+        for h in range(2):
+            z, tok = T.z3[:, 512 * h:512 * h + 512], "z3e%d z3o%d" % (h, h)
+            tt(z, z, T.q4ps[:, 512 * h:512 * h + 512], OP.subtract, tok, tok + " qp%d" % h)
+        pair(3, ("z3e0 z3e1", "z3o0 z3o1"))
+        fused(1, None, "z1e z1o")
+        pair(1, ("z1e", "z1o"))
         fused(2, 0, "z2a")
         absz(T.z2[:, 0:512], "z2a")
         fused(2, 1, "z2e z2o")
         absz(T.z2[:, 512::2], "z2e")
-        mms(sums(2, ALL[0::2], False), "z2a z2e W65", "D2")
+        sums(2, ALL[0::2], False, "z2a z2e")
         absz(T.z2[:, 513::2], "z2o")
-        mms(sums(2, ALL[1::2], True), "z2a z2o W65", "D2")
+        sums(2, ALL[1::2], True, "z2a z2o")
 
-    def scan(ch):
-        op("v", lambda e: e.tensor_tensor_scan(out=T["SC%d" % ch][:], data0=T.RST[:], data1=T["D%d" % ch][:, 0:64],
-                                               initial=BIG, op0=OP.max, op1=OP.min), "RST", "SC%d D%d" % (ch, ch))
+    def scan(b):
+        op("v", lambda e: e.tensor_tensor_scan(out=T["S" + b][:], data0=T["RS" + b][:], data1=T["D" + b][:, 0:256 if b == "A" else 64],
+                                               initial=BIG, op0=OP.max, op1=OP.min), "RS" + b, "S%s D%s" % (b, b))
 
-    def scans01():
-        scan(0)
-        scan(1)
-        tt(T.M[:], T.SC0[:, 3::4], T.SC1[:, 3::4], OP.min, "SC0 SC1", "M")
-
-    def scans32(k):
-        scan(3)
-        tt(T.M[:], T.M[:], T.SC3[:, 3::4], OP.min, "M SC3", "M")
-        if k < NR - 1:
-            tt(T.Mu[:], T.M[:], T["u%d" % (k + 1)][:], OP.min, "M u%d" % (k + 1), "Mu")
-        scan(2)
+    MA, MB = T.SA[:, 15::16], T.SB[:, 3::4]
 
     def chain(k):
-        tt(T.t1[:], T.Mu[:], T.SC2[:, 3::4], OP.min, "Mu SC2", "t1")
+        tt(T.t1[:], T.Mu[:], MB, OP.min, "Mu SB", "t1")
         tt(T.t2[:], T.t1[:], T["w%d" % k][:], OP.max, "t1 w%d" % k, "t2")
         ts(T.bi[:], T.t2[:], 4095, None, OP.bitwise_and, None, "t2", "bi")
         cp(T.bh[:], T.bi[:], "bi", "bh")
-        tt(T.bl[:], T.bi[:], T.bh[:], OP.subtract, "bi bh", "bl")
-        mms(conv("bh", "bl", 0, "CV"), "bh bl Ev Od", "CV")
         cp(T.bu[:], T.bi[:], "bi", "bu")
-        qpart(k, T.bu[:], "bu")
+        tt(T.bl[:], T.bi[:], T.bh[:], OP.subtract, "bi bh", "bl")
+        mms(conv("bh", "bl", "CV"), "bh bl Ev Od", "CV")
+        qpart(k, T.bu, "bu")
 
     def keys(k):
-        tt(kk("K", k), T.M[:], T.SC2[:, 3::4], OP.min, "M SC2", "K%d" % k)
-        ts(kk("B", k), kk("K", k), 4095, None, OP.bitwise_and, None, "K%d" % k, "B%d" % k)
         tc = T.Tk[:, k:k + 1]
+        r = [lambda: tt(kk("K", k), MA, MB, OP.min, "SA SB", "K%d" % k),
+             lambda: ts(kk("B", k), kk("K", k), 4095, None, OP.bitwise_and, None, "K%d" % k, "B%d" % k)]
         if k == 0:
-            ts(kk("lv", 0), kk("K", 0), tc, None, OP.is_lt, None, "K0 Tk", "lv0")
+            r.append(lambda: ts(kk("lv", 0), kk("K", 0), tc, None, OP.is_lt, None, "K0 Tk", "lv0"))
         else:
-            ts(T.lt[:], kk("K", k), tc, None, OP.is_lt, None, "K%d Tk" % k, "lt")
-            tt(kk("lv", k), T.lt[:], T["g%d" % k][:], OP.mult, "lt g%d" % k, "lv%d" % k)
-        tt(T.yo[:], kk("B", k), kk("lv", k), OP.mult, "B%d lv%d" % (k, k), "yo")
-        cp(kk("yu", k), T.yo[:], "yo", "yu%d" % k)
+            r.append(lambda: ts(T.lt[:], kk("K", k), tc, None, OP.is_lt, None, "K%d Tk" % k, "lt"))
+            r.append(lambda: tt(kk("lv", k), T.lt[:], T["g%d" % k][:], OP.mult, "lt g%d" % k, "lv%d" % k))
+        r.append(lambda: tt(T.yo[:], kk("B", k), kk("lv", k), OP.mult, "B%d lv%d" % (k, k), "yo"))
+        r.append(lambda: cp(kk("yu", k), T.yo[:], "yo", "yu%d" % k))
+        return r
 
-    def rewire_pre(t, k):
-        P, ptok = (T.Er, "Er") if k == 0 else (T["P%dr" % k], "P%dr" % k)
-        if k == 1:
-            tt(T.px[:], kk("B", 0), T.Ep[:], OP.subtract, "B0 Ep", "px")
-            tt(T.px[:], T.px[:], kk("lv", 0), OP.mult, "px lv0", "px")
-            tt(T.P1p[:], T.px[:], T.Ep[:], OP.add, "px Ep", "P1p")
-            tt(T.P1r[:], T.px[:], T.Er[:], OP.add, "px Er", "P1r")
-        if k == 2:
-            tt(T.px[:], kk("B", 1), T.P1p[:], OP.subtract, "B1 P1p", "px")
-            tt(T.px[:], T.px[:], kk("lv", 1), OP.mult, "px lv1", "px")
-            tt(T.P2r[:], T.px[:], T.P1r[:], OP.add, "px P1r", "P2r")
-        tt(T.rz[:], kk("LA", k), P[:], OP.mult, "LA%d %s" % (k, ptok), "rz")
-        z, ztok = T.rz, "rz"
-        if k:
-            ts(T.rz2[:], T.rz[:], 32.0 * k, None, OP.add, None, "rz", "rz2")
-            z, ztok = T.rz2, "rz2"
-        ts(T.NW[:, 0:16], z[:], 5, 2047, OP.arith_shift_right, OP.bitwise_and, ztok, "NW0")
-        if k == 1:
-            ts(T.NW[:, 16:32], kk("lv", 0), -1.0, None, OP.add, None, "lv0", "NW1")
-        if k == 2:
-            ts(T.p2[:], kk("lv", 1), 2.0, -1.0, OP.mult, OP.add, "lv1", "p2")
-            ts(T.ga[:], kk("lv", 0), -1.0, None, OP.add, None, "lv0", "ga")
-            tt(T.NW[:, 16:32], T.p2[:], T.ga[:], OP.max, "p2 ga", "NW1")
-        n = 32 if k else 16
-        tt(T.df[:, 0:n], T.NW[:, 0:n], T["land_%d" % k][:, 32 * t:32 * t + n], OP.subtract,
-           "NW0 land%d_%d" % (t, k) + (" NW1" if k else ""), "df")
-
-    def rewire(t, k):
-        n = 32 if k else 16
-        for h in range(n // 16):
-            act(T.dd[:, 16 * h:16 * h + 16], kk("lv", k), ACT.Copy, "lv%d" % k, "dd%d" % h, bias=1.0, scale=-1.0)
-        tt(T.df[:, 0:n], T.df[:, 0:n], T.dd[:, 0:n], OP.mult, "df dd0" + (" dd1" if k else ""), "df")
-        src = T["src_%d" % k][:, 32 * t:32 * t + n]
-        tt(src, T.df[:, 0:n], T["land_%d" % k][:, 32 * t:32 * t + n], OP.add, "df land%d_%d" % (t, k), "src%d_%d" % (t, k))
+    def send(t, w, src, dst_ap):
         dst = T.cores[(rank + 1) % n_ranks if t < NV - 1 else (rank - t) % n_ranks]
-        before("g", ["src%d_%d" % (t, k)], [])
+        before("g", ["src%d_%d" % (t, w)], [])
         rid, pid = topo.addr(dst, core)
-        ar = "ar%d_%d" % (t + 1, k)
-        g.remote_dma(T["land_%d" % k][:, 32 * (t + 1):32 * (t + 1) + n], src, T.sem[ar], T.sem.ls, pid, rid, topo.mask(core, dst))
+        ar = "ar%d_%d" % (t + 1, w)
+        g.remote_dma(dst_ap, src, T.sem[ar], T.sem.ls, pid, rid, topo.mask(core, dst))
         ne = len(topo.engines(core, dst))
         sent[0] += ne
-        lastw["land%d_%d" % (t + 1, k)] = (ar, ne, "remote")
+        lastw["land%d_%d" % (t + 1, w)] = (ar, ne, "remote")
+
+    def rewire0_pre(t):
+        tt(T.rz0[:], kk("LA", 0), T.Er[:], OP.mult, "LA0 Er", "rz0")
+        ts(T.NW0[:], T.rz0[:], 5, 2047, OP.arith_shift_right, OP.bitwise_and, "rz0", "NW0")
+        tt(T.df0[:], T.NW0[:], T.land0[:, 16 * t:16 * t + 16], OP.subtract, "NW0 land%d_0" % t, "df0")
+
+    def rewire0(t):
+        tt(T.x0[:], T.df0[:], kk("lv", 0), OP.mult, "df0 lv0", "x0")
+        src = T.src0[:, 16 * t:16 * t + 16]
+        tt(src, T.NW0[:], T.x0[:], OP.subtract, "NW0 x0", "src%d_0" % t)
+        send(t, 0, src, T.land0[:, 16 * t + 16:16 * t + 32])
+
+    def rewire1_p1():
+        return [lambda: tt(T.px[:], kk("B", 0), T.Ep[:], OP.subtract, "B0 Ep", "px"),
+                lambda: tt(T.px[:], T.px[:], kk("lv", 0), OP.mult, "px lv0", "px"),
+                lambda: ts(T.NW[:, 32:48], kk("lv", 0), -1.0, None, OP.add, None, "lv0", "NWp1"),
+                lambda: tt(T.P12[:, 0:16], T.px[:], T.Ep[:], OP.add, "px Ep", "P1")]
+
+    def rewire1_pre(t):
+        return [lambda: tt(T.qx[:], kk("B", 1), T.P12[:, 0:16], OP.subtract, "B1 P1", "qx"),
+                lambda: tt(T.qx[:], T.qx[:], kk("lv", 1), OP.mult, "qx lv1", "qx"),
+                lambda: tt(T.P12[:, 16:32], T.qx[:], T.P12[:, 0:16], OP.add, "qx P1", "P2"),
+                lambda: tt(T.NW[:, 48:64], T.pa[:], T.pb[:], OP.max, "pa pb", "NWp2"),
+                lambda: tt(T.rz12[:], T.LA[:, 16:48], T.P12[:], OP.mult, "LA1 P1 P2", "rz12"),
+                lambda: tt(T.rk12[:], T.rz12[:], T.LAk[:], OP.add, "rz12 LAk1 LAk2", "rk12"),
+                lambda: ts(T.NW[:, 0:32], T.rk12[:], 5, 2047, OP.arith_shift_right, OP.bitwise_and, "rk12", "NWl"),
+                lambda: tt(T.df[:], T.NW[:], T.land1[:, 64 * t:64 * t + 64], OP.subtract, "NWl NWp1 NWp2 land%d_1" % t, "df")]
+
+    def rewire1(t):
+        src = T.src1[:, 64 * t:64 * t + 64]
+        return [lambda: tt(T.xx[:], T.df[:], T.lvd[:], OP.mult, "df lvd0 lvd1", "xx"),
+                lambda: tt(src, T.NW[:], T.xx[:], OP.subtract, "NWl NWp1 NWp2 xx", "src%d_1" % t),
+                lambda: send(t, 1, src, T.land1[:, 64 * t + 64:64 * t + 128])]
 
     def thresholds():
-        mms([(T.CV[:, 0:48], T.oneb[:], T.lv[:], True, True)], "oneb lv0 lv1 lv2", "CV")
-        op("v", lambda e: e.tensor_reduce(out=T.cnt[:], in_=T.CV[:, 0:48], axis=AxisListType.X, op=OP.add), "", "cnt CV")
-        ts(T.ai[:], T.cnt[:], -1.0, 6144.0, OP.mult, OP.add, "cnt", "ai")
-        ts(T.ai2[:], T.ai[:], 31, None, OP.bitwise_and, None, "ai", "ai2")
-        ts(T.af[:], T.ai2[:], 65536.0, None, OP.mult, None, "ai2", "af")
-        ts(T.Tk[:], T.thk[:], T.af[:], None, OP.add, None, "thk af", "Tk")
+        return [lambda: op("v", lambda e: e.tensor_reduce(out=T.cnt[:], in_=T.CV[:, 0:48], axis=AxisListType.X, op=OP.add), "", "cnt CV"),
+                lambda: ts(T.ai[:], T.cnt[:], -1.0, 6144.0, OP.mult, OP.add, "cnt", "ai"),
+                lambda: ts(T.ai2[:], T.ai[:], 31, None, OP.bitwise_and, None, "ai", "ai2"),
+                lambda: ts(T.af[:], T.ai2[:], 65536.0, None, OP.mult, None, "ai2", "af"),
+                lambda: ts(T.Tk[:], T.thk[:], T.af[:], None, OP.add, None, "thk af", "Tk")]
 
     ts(T.Ep[:], T.exi[:], float(PAD), None, OP.add, None, "exi", "Ep")
     cp(T.eh[:], T.Ep[:], "Ep", "eh")
     tt(T.el[:], T.Ep[:], T.eh[:], OP.subtract, "Ep eh", "el")
-    mms(conv("eh", "el", 0, "CV"), "eh el Ev Od", "CV")
+    mms(conv("eh", "el", "CV"), "eh el Ev Od", "CV")
     act(T.Es[:], T.CV[:, 0:16], ACT.Copy, "", "CV Es")
-    cp(T.land_0[:, 0:16], T.lci[:, 0:16], "lci", "land0_0")
-    arr_s(0, 0)
-    arr_v(0, 0)
-    cp(T.Er[:], T.exi[:], "exi", "Er")
+    cp(T.land0[:, 0:16], T.lci[:, 0:16], "lci", "land0_0")
     cp(T.Eu[:], T.Ep[:], "Ep", "Eu")
+    arr_s(0, 0)
+    arr_u(0, 0)
+    arr_l(0)
+    arr_e(0)
+    xl(0, HALVES)
+    cp(T.Er[:], T.exi[:], "exi", "Er")
     ts(T.W65[:], T.W[:], 65536.0, None, OP.mult, None, "W", "W65")
     cp(T.IB[:], T.I32[:], "I32", "IB")
-    ts(T.RST[:], T.RST[:], BIG, None, OP.mult, None, "RST", "RST")
-    npart(0, 0, T.Es[:], "Es")
-    xl(0)
+    ts(T.RSA[:], T.RSA[:], BIG, None, OP.mult, None, "RSA", "RSA")
+    ts(T.RSB[:], T.RSB[:], BIG, None, OP.mult, None, "RSB", "RSB")
+    fill(T.MK[0:1, 2::4], BIG, "MK")
+    np_ = npart(0, 0, T.Es[:], "Es")
+    weave(np_[0:4], [])
+    qpart(0, T.Eu, "Eu", HALVES)
+    cp(T.land1[:, 0:32], T.lci[:, 16:48], "lci", "land0_1")
+    ts(T.tsel[:], T.tsel[:], 65536.0, None, OP.mult, None, "tsel", "tsel")
+    ts(T.base[:], T.b128[:], T.p8[:], None, OP.add, None, "b128 p8", "base")
+    fill(T.mone[:], -1.0, "mone")
+    dma("y", T.yi[:, 0:16], T.mone[:], "dout", 64, "mone", "yi0")
+    weave(np_[4:], [])
+    cp(T.land1[:, 32:64], T.upi[:, 16:48], "upi", "land0_1")
+    cp(T.thf[:], T.thi[:], "thi", "thf")
+    cp(T.wtf[:], T.wti[:], "wti", "wtf")
+    ts(T.SW[:], T.W[:], T.wtf[:], None, OP.mult, None, "W wtf", "SW")
+    for b in range(2):
+        dma("y", T.FA[:, b * FW + 1024:(b + 1) * FW], T.FA[:, b * FW:b * FW + FW - 1024], "dfw", 32, FAtok, "FAx%d" % b)
 
     for t in range(NV):
-        qpart(0, T.Eu[:], "Eu")
+        more = t < NV - 1
+        main()
         if t == 0:
-            for b in range(2):
-                dma("y", T.FA[:, b * FW + 1024:(b + 1) * FW], T.FA[:, b * FW:b * FW + FW - 1024], "dfw", 32, FAtok, "FAx%d" % b)
-            for k in (1, 2):
-                cp(T["land_%d" % k][:, 0:16], T.lci[:, 16 * k:16 * k + 16], "lci", "land0_%d" % k)
-                cp(T["land_%d" % k][:, 16:32], T.upi[:, 16 * k:16 * k + 16], "upi", "land0_%d" % k)
-            cp(T.thf[:], T.thi[:], "thi", "thf")
-            ts(T.tsel[:], T.tsel[:], 65536.0, None, OP.mult, None, "tsel", "tsel")
             mms([(T.MS[:, 0:3], T.tsel[:], T.thf[:], True, True)], "tsel thf", "MS")
             act(T.thk[:], T.MS[:, 0:3], ACT.Copy, "", "MS thk")
             act(T.Tk[:], T.thk[:], ACT.Copy, "thk", "Tk")
-            cp(T.wtf[:], T.wti[:], "wti", "wtf")
-            ts(T.SW[:], T.W[:], T.wtf[:], None, OP.mult, None, "W wtf", "SW")
-            ts(T.base[:], T.b128[:], T.p8[:], None, OP.add, None, "b128 p8", "base")
-            fill(T.mone[:], -1.0, "mone")
-            dma("y", T.yi[:, 0:16], T.mone[:], "dout", 96, "mone", "yi0")
-        else:
-            rewire_pre(t - 1, 1)
-            rewire(t - 1, 1)
-            rewire_pre(t - 1, 2)
-            rewire(t - 1, 2)
-            thresholds()
-        main(0)
+        arr_u(t, 1)
         arr_s(t, 1)
-        arr_v(t, 1)
-        masks(t, 1)
+        masks1(t)
         xl(1)
-        scans01()
-        rewire_pre(t, 0)
-        scans32(0)
+        rewire0_pre(t)
+        scan("A")
+        arr_l(1)
+        masks2(t)
+        arr_e(1)
+        tt(T.w1[:], T.n12[:, 0:16], T.Ep[:], OP.mult, "n12 Ep", "w1")
+        tt(T.Mu[:], MA, T.u1[:], OP.min, "SA u1", "Mu")
+        tt(T.nE[:], T.n12[:, 16:32], T.Ep[:], OP.mult, "n12 Ep", "nE")
+        scan("B")
         chain(1)
-        npart(t, 1, T.CV[:, 0:16], "CV")
-        main(1)
-        keys(0)
-        act(T.y0[:], Xw.indirect(kk("yu", 0)), ACT.Copy, "X Xpad yu0", "y0")
-        rewire(t, 0)
-        arr_s(t, 2)
-        arr_v(t, 2)
+        ks = keys(0)
+        weave(ks[0:2], [])
+        weave(npart(t, 1, T.CV[:, 0:16], "CV"), ks[2:])
+        main()
         xl(2)
-        masks(t, 2)
+        act(T.y0[:], Xw.indirect(kk("yu", 0)), ACT.Copy, "X Xpad yu0", "y0")
+        rewire0(t)
         tt(T.sB[:], T.s20[:], kk("B", 0), OP.mult, "s20 B0", "sB")
-        tt(T.w2[:], T.sB[:], T.nE[:], OP.add, "sB nE", "w2")
-        scans01()
-        tt(T.g1[:], T.n1[:], kk("lv", 0), OP.max, "n1 lv0", "g1")
-        scans32(1)
+        scan("A")
+        weave([lambda: tt(T.w2[:], T.sB[:], T.nE[:], OP.add, "sB nE", "w2"),
+               lambda: tt(T.Mu[:], MA, T.u2[:], OP.min, "SA u2", "Mu"),
+               lambda: tt(T.g1[:], T.n12[:, 0:16], kk("lv", 0), OP.max, "n12 lv0", "g1"),
+               lambda: tt(T.ga[:], T.s20[:], kk("lv", 0), OP.mult, "s20 lv0", "ga")], rewire1_p1())
+        scan("B")
         chain(2)
-        npart(t, 2, T.CV[:, 0:16], "CV")
-        main(2)
-        keys(1)
-        tt(T.y01[:], Xw.indirect(kk("yu", 1)), T.y0[:], OP.max, "X Xpad yu1 y0", "y01")
-        if t < NV - 1:
+        ks = keys(1)
+        weave(ks[0:2], [])
+        weave(npart(t, 2, T.CV[:, 0:16], "CV"), ks[2:])
+        main()
+        if more:
+            arr_u(t + 1, 0)
             arr_s(t + 1, 0)
-            arr_v(t + 1, 0)
-        tt(T.ga[:], T.s20[:], kk("lv", 0), OP.mult, "s20 lv0", "ga")
+        act(T.pb[:], kk("lv", 0), ACT.Copy, "lv0", "pb", bias=-1.0)
+        act(T.pa[:], kk("lv", 1), ACT.Copy, "lv1", "pa", scale=2.0, bias=-1.0)
         tt(T.gb[:], T.s21[:], kk("lv", 1), OP.mult, "s21 lv1", "gb")
-        tt(T.ga[:], T.ga[:], T.gb[:], OP.max, "ga gb", "ga")
-        tt(T.g2[:], T.ga[:], T.n2[:], OP.max, "ga n2", "g2")
-        scans01()
-        scans32(2)
-        keys(2)
+        tt(T.ga[:], T.ga[:], T.n12[:, 16:32], OP.max, "ga n12", "ga")
+        tt(T.y01[:], Xw.indirect(kk("yu", 1)), T.y0[:], OP.max, "X Xpad yu1 y0", "y01")
+        scan("A")
+        weave([lambda: tt(T.g2[:], T.ga[:], T.gb[:], OP.max, "ga gb", "g2"),
+               (lambda: (arr_l(0), arr_e(0))) if more else None], rewire1_pre(t))
+        scan("B")
+        np_ = npart(t + 1, 0, T.Es[:], "Es") if more else []
+        weave(keys(2), [None] * 3 + np_[0:4])
+        for h in range(2):
+            act(T.lvd[:, 32 * h:32 * h + 32], T.lv[:, 16:48], ACT.Copy, "lv1 lv2", "lvd%d" % h)
         tt(T.yy[:], Xw.indirect(kk("yu", 2)), T.y01[:], OP.max, "X Xpad yu2 y01", "yy")
         mms([(T.CV[:, 0:16], T.SW[:, 15 - p:143 - p], T.yy[:, p::16], p == 0, p == 15) for p in ALL], "SW yy", "CV")
-        if t < NV - 1:
-            npart(t + 1, 0, T.Es[:], "Es")
+        weave(np_[4:], [])
+        put = [lambda: cp(T.si[:], T.CV[:, 0:16], "", "si CV"),
+               lambda: ts(T.sm[:], T.si[:], 7, None, OP.bitwise_and, None, "si", "sm"),
+               lambda: tt(T.sa[:], T.sm[:], T.base[:], OP.add, "sm base", "sa")]
+        if more:
+            put.append(lambda: cp(T.wu[:], T.sa[:], "sa", "wu"))
+            weave(put, rewire1(t))
+            op("v", lambda e: e.tensor_copy(out=Xw.indirect(T.wu[:]), in_=T.yy[:]), "wu yy", "X Xpad")
+            xl(0, HALVES)
+            mms([(T.CV[:, 0:48], T.oneb[:], T.lv[:], True, True)], "oneb lv0 lv1 lv2", "CV")
+            th = thresholds()
+            weave(th[0:3], [])
+            qpart(0, T.Eu, "Eu", HALVES)
+            weave(th[3:], [])
         else:
-            rewire_pre(t, 1)
-            rewire(t, 1)
-            rewire_pre(t, 2)
-            rewire(t, 2)
-        cp(T.si[:], T.CV[:, 0:16], "", "si CV")
-        ts(T.sm[:], T.si[:], 7, None, OP.bitwise_and, None, "si", "sm")
-        tt(T.sa[:], T.sm[:], T.base[:], OP.add, "sm base", "sa")
-        cp(T.wu[:], T.sa[:], "sa", "wu")
-        op("v", lambda e: e.tensor_copy(out=Xw.indirect(T.wu[:]), in_=T.yy[:]), "wu yy", "X Xpad")
-        if t < NV - 1:
-            xl(0)
+            weave(rewire1(t), put)
+            M = PAD + 1024
+            cp(T.wu[:, 0:8], T.sa[:, 0:8], "sa", "wu0")
+            ts(T.wu[:, 8:16], T.sa[:, 8:16], float(-M), None, OP.add, None, "sa", "wu1")
+            op("v", lambda e: e.tensor_copy(out=T.X[:, 0:M].indirect(T.wu[:, 0:8]), in_=T.yy[:, 0:128]), "wu0 yy X", "Xpad")
+            op("v", lambda e: e.tensor_copy(out=T.X[:, M:M + 1024].indirect(T.wu[:, 8:16]), in_=T.yy[:, 128:256]), "wu1 yy", "X")
+            dma("s", T.yx[:, 0:1024], T.X[:, PAD:M], "dy", 32, "Xpad", "yxo0")
+            dma("s", T.yx[:, 1024:2048], T.X[:, M:M + 1024], "dy", 32, "X", "yxo1")
 
-    dma("s", T.yx[:], T.X[:, PAD:PAD + 2048], "dx", 32, "X Xpad", "yxo")
-    for k in range(NR):
-        tok = "land%d_%d" % (NV, k)
-        dma("y", T.yl[:, 16 * k:16 * k + 16], T["land_%d" % k][:, 32 * NV:32 * NV + 16], "dout", 96, tok, "ylo%d" % k)
-        if k:
-            dma("y", T.yi[:, 16 * k:16 * k + 16], T["land_%d" % k][:, 32 * NV + 16:32 * NV + 32], "dout", 96, tok, "yio%d" % k)
-    need("g", "dout", 96)
-    need("g", "dx", 32)
+    dma("y", T.yl[:, 0:16], T.land0[:, 16 * NV:16 * NV + 16], "dout", 64, "land%d_0" % NV, "ylo0")
+    dma("y", T.yl[:, 16:48], T.land1[:, 64 * NV:64 * NV + 32], "dout", 64, "land%d_1" % NV, "ylo1")
+    dma("y", T.yi[:, 16:48], T.land1[:, 64 * NV + 32:64 * NV + 64], "dout", 64, "land%d_1" % NV, "yio1")
+    need("g", "dout", 64)
+    need("g", "dy", 32)
     need("g", "ls", sent[0])
     for q in ("v", "s", "p", "g"):
         need("g", "c" + q, count[q])

from concourse.mybir import dt, AluOpType, AxisListType, ActivationFunctionType

OP = AluOpType
ACT = ActivationFunctionType
NV, NR, PAD, FW = 4, 3, 32, 1264
BIG = 16777216.0
ROT = 864

SCRATCH = {}


def _decl(where, dtype, names, n, rows=128):
    for nm in names.split():
        SCRATCH[nm] = (where, [rows, n], dtype)


_decl("sbuf", "bfloat16", "X", 2080)
_decl("sbuf", "int32", "FA", 2 * FW)
_decl("sbuf", "float32", "C CT SA RSA onef", 256)
_decl("sbuf", "uint16", "CTu", 256)
_decl("sbuf", "bfloat16", "qq yy y0 y01", 256)
_decl("sbuf", "bfloat16", "Q4 z0 z1 z2 z3", 1024)
_decl("psum", "float32", "q4ps", 1024)
_decl("psum", "float32", "CV MS DA DB", 512)
_decl("sbuf", "float32", "SB RSB", 64)
_decl("sbuf", "int32", "EXi", 32)
_decl("sbuf", "uint16", "EXu", 32)
_decl("sbuf", "int32", "lci upi", 48)
_decl("sbuf", "int32", "thi", 3, 8)
_decl("sbuf", "float32", "thf", 3, 8)
_decl("sbuf", "float32", "tsel", 128, 8)
_decl("sbuf", "bfloat16", "MK", 256, 1)
_decl("sbuf", "bfloat16", "MK2", 64, 1)
_decl("sbuf", "int32", "wti ai ai2 pi pg p15", 1)
_decl("sbuf", "float32", "wtf cnt af par p8 p15f", 1)
_decl("sbuf", "float32", "thk Tk", 3)
_decl("sbuf", "float32", "nc", 8)
_decl("sbuf", "float32", "D160", 160)
_decl("sbuf", "bfloat16", "Ev Od", 160)
_decl("sbuf", "float32", "W", 144)
_decl("sbuf", "bfloat16", "W65 SW", 144)
_decl("sbuf", "float32", "I32", 128)
_decl("sbuf", "bfloat16", "IB oneb", 128)
_decl("sbuf", "int32", "exi b128 base z32 nn t2 bi rz0 NW0 si sm sa", 16)
_decl("sbuf", "uint16", "Eu nu bu wu", 16)
_decl("sbuf", "bfloat16", "eh el bh bl lt", 16)
_decl("sbuf", "float32", "mone Ep Er Es Mu t1 yo u1 w1 u2 w2 s20 s21 nE sB g1 g2 ga gb px qx df0 x0 a2 pa pb", 16)
_decl("sbuf", "float32", "n12 P12 LAk rz12", 32)
_decl("sbuf", "int32", "rk12", 32)
_decl("sbuf", "int32", "NW", 64)
_decl("sbuf", "float32", "df xx lvd", 64)
_decl("sbuf", "bfloat16", "lv Lh Ll", 48)
_decl("sbuf", "uint16", "Lu yu", 48)
_decl("sbuf", "float32", "LA LS", 48)
_decl("sbuf", "int32", "K B", 48)
_decl("sbuf", "bfloat16", "XL", 768)
_decl("sbuf", "float32", "land0", 5 * 16)
_decl("sbuf", "float32", "land1", 5 * 64)
_decl("sbuf", "float32", "src0", 4 * 16)
_decl("sbuf", "float32", "src1", 4 * 64)

SEMAPHORES = ["cv", "cs", "cp", "cg", "ls", "dfa", "dfw", "dx", "dy", "dlc", "dup", "dex", "dth", "dwt", "dout"]
SEMAPHORES += ["ar%d_%d" % (t, k) for t in range(1, 5) for k in range(2)]


def rank_program(g, core, T, topo):
    rank = T.rank_of(core)
    if rank is None:
        return
    n_ranks = len(T.cores)
    QUEUE = {"v": g.vector, "s": g.scalar, "p": g.tensor, "g": g, "y": g.sync}
    count = {"v": 0, "s": 0, "p": 0, "g": 0}
    known = {q: {} for q in QUEUE}
    snap, lastw, readers, sent = {}, {}, {}, [0]

    def need(q, sem, val):
        if known[q].get(sem, 0) >= val:
            return
        QUEUE[q].wait_ge(T.sem[sem], val)
        for s_, v_ in snap.get((sem, val), {}).items():
            if known[q].get(s_, 0) < v_:
                known[q][s_] = v_
        known[q][sem] = val

    def before(q, r, w):
        deps = {}

        def add(d):
            if deps.get(d[0], 0) < d[1]:
                deps[d[0]] = d[1]
        for b in r:
            if b in lastw:
                add(lastw[b])
        for b in w:
            if b in lastw and not (lastw[b][2] == q and q == "p"):
                add(lastw[b])
            for d in readers.get(b, ()):
                if d[2] != q:
                    add(d)
        for sem in sorted(deps, key=lambda s_: -len(snap.get((s_, deps[s_]), {}))):
            need(q, sem, deps[sem])

    def after(q, sem, val, r, w):
        d = (sem, val, q)
        for b in r:
            readers.setdefault(b, []).append(d)
        for b in w:
            lastw[b] = d
            readers[b] = []
        snap[(sem, val)] = dict(known[q])

    def op(q, fn, r, w):
        r, w = r.split(), w.split()
        before(q, r, w)
        ins = fn(QUEUE[q])
        count[q] += 1
        ins.then_inc(T.sem["c" + q], 1)
        after(q, "c" + q, count[q], r, w)

    def dma(q, out, in_, sem, total, r, w):
        r, w = r.split(), w.split()
        before(q, r, w)
        QUEUE[q].dma_start(out=out, in_=in_).then_inc(T.sem[sem], 16)
        after(q, sem, total, r, w)

    def tt(o, a, b, f, r, w):
        op("v", lambda e: e.tensor_tensor(out=o, in0=a, in1=b, op=f), r, w)

    def ts(o, a, s1, s2, f0, f1, r, w):
        if s2 is None:
            op("v", lambda e: e.tensor_scalar(out=o, in0=a, scalar1=s1, scalar2=None, op0=f0), r, w)
        else:
            op("v", lambda e: e.tensor_scalar(out=o, in0=a, scalar1=s1, scalar2=s2, op0=f0, op1=f1), r, w)

    def cp(o, a, r, w):
        op("v", lambda e: e.tensor_copy(out=o, in_=a), r, w)

    def fill(o, c, w):
        op("v", lambda e: e.memset(o, c), "", w)

    def act(o, a, f, r, w, bias=0.0, scale=1.0):
        op("s", lambda e: e.activation(out=o, in_=a, func=f, bias=bias, scale=scale), r, w)

    def mms(lst, r, w):
        def fn(e):
            ins = None
            for (o, a, b, st, sp) in lst:
                ins = e.matmul(out=o, lhsT=a, rhs=b, start=st, stop=sp)
            return ins
        op("p", fn, r, w)

    def kk(nm, k):
        return T[nm][:, 16 * k:16 * k + 16]

    def weave(a, b):
        for i in range(max(len(a), len(b))):
            for l in (a, b):
                if i < len(l) and l[i]:
                    l[i]()

    Xw = T.X[:, 0:2080]

    dma("y", T.exi[:], T.ex[:], "dex", 16, "", "exi")
    dma("s", T.lci[:], T.lc[:], "dlc", 16, "", "lci")
    dma("y", T.X[:, PAD:PAD + 2048], T.xs[:], "dx", 16, "", "X")
    it = [0]

    def lfa(rows, src, blk):
        for (a, b, c) in ((0, ROT, 1024), (1024 - ROT, 0, ROT)):
            q = "sy"[it[0] % 2]
            it[0] += 1
            dma(q, T.FA[rows, blk * FW + a:blk * FW + a + c - b], T.fa[src, b:c], "dfa", 288, "", "FA%d" % it[0])
    lfa(slice(0, 128), slice(0, 128), 0)
    for G in range(8):
        o = G ^ 1
        lfa(slice(16 * G, 16 * G + 16), slice(16 * o, 16 * o + 16), 1)
    FAtok = " ".join("FA%d" % (i + 1) for i in range(it[0]))
    dma("y", T.upi[:], T.up[:], "dup", 16, "", "upi")
    dma("y", T.thi[:], T.th[:], "dth", 16, "", "thi")
    dma("y", T.wti[:], T.wt[:], "dwt", 16, "", "wti")

    fill(T.onef[:], 1.0, "onef")
    op("g", lambda e: e.iota(T.pi[:], [[0, 1]], 0, 1), "", "pi")

    def aff(o, a, pat, f, base, cm, r, w):
        op("g", lambda e: e.affine_select(o, a, pat, f, 0.0, base, cm), r, w)

    def iob(o, pat, base, w):
        op("g", lambda e: e.iota(o, pat, base, 0, allow_small_or_imprecise_dtypes=True), "", w)
    aff(T.D160[:], T.onef[:, 0:160], [[-1, 160]], OP.is_equal, 16, 1, "onef", "D160")
    op("g", lambda e: e.iota(T.EXi[:], [[16, 8], [0, 4]], 0, 0), "", "EXi")
    aff(T.I32[:], T.onef[:, 0:128], [[-1, 128]], OP.is_equal, 0, 1, "onef", "I32")
    iob(T.MK[0:1, :], [[0, 16], [4096, 16]], 0, "MK")
    iob(T.MK2[0:1, :], [[0, 16], [16384, 4]], 8192, "MK2")
    aff(T.W[:], T.onef[:, 0:144], [[-16, 9], [0, 16]], OP.is_ge, 0, 1, "onef", "W")
    aff(T.W[:], T.W[:], [[16, 9], [0, 16]], OP.is_ge, 15, -1, "W", "W")
    aff(T.W[:], T.W[:], [[0, 9], [1, 16]], OP.is_equal, -15, 0, "W", "W")
    aff(T.RSA[:], T.onef[:], [[0, 16], [1, 16]], OP.is_equal, 0, 0, "onef", "RSA")
    aff(T.RSB[:], T.onef[:, 0:64], [[0, 16], [1, 4]], OP.is_equal, 0, 0, "onef", "RSB")
    op("g", lambda e: e.iota(T.b128[:], [[128, 16]], PAD, 0), "", "b128")
    aff(T.tsel[:], T.onef[0:8, 0:128], [[1, 128]], OP.is_ge, 0, -16, "onef", "tsel")
    aff(T.tsel[:], T.tsel[:], [[-1, 128]], OP.is_ge, 15, 16, "tsel", "tsel")

    fill(T.FA[:, 1024:FW], 0, "FAx0")
    fill(T.FA[:, FW + 1024:2 * FW], 0, "FAx1")
    fill(T.X[:, 0:PAD], 0.0, "Xpad")
    fill(T.oneb[:], 1.0, "oneb")
    ts(T.pg[:], T.pi[:], 4, 1, OP.arith_shift_right, OP.bitwise_and, "pi", "pg")
    ts(T.p15[:], T.pi[:], 15, None, OP.bitwise_and, None, "pi", "p15")
    cp(T.par[:], T.pg[:], "pg", "par")
    cp(T.p15f[:], T.p15[:], "p15", "p15f")
    ts(T.p8[:], T.p15f[:], 8.0, None, OP.mult, None, "p15f", "p8")
    ts(T.EXu[:], T.EXi[:], T.p15f[:], None, OP.add, None, "EXi p15f", "EXu")
    REM = [(77 * t) % 8 for t in range(NV)]
    for t in range(NV):
        ts(T.nc[:, 2 * t:2 * t + 1], T.par[:], float(FW), float(REM[t]), OP.mult, OP.add, "par", "nc%d" % (2 * t))
        ts(T.nc[:, 2 * t + 1:2 * t + 2], T.par[:], float(-FW), float(FW + REM[t]), OP.mult, OP.add, "par",
           "nc%d" % (2 * t + 1))
    for h, nm in ((1, "Ev"), (0, "Od")):
        cp(T[nm][:], T.D160[:], "D160", nm)
        for b in range(10):
            if b % 2 != h:
                fill(T[nm][:, 16 * b:16 * b + 16], 0.0, nm)

    MAT = {(0, 0): T.Ev[:, 16:144], (0, 1): T.Ev[:, 0:128], (1, 1): T.Od[:, 16:144], (1, 0): T.Od[:, 32:160]}

    def conv(h, l, bank, a=0, e=16):
        lst, n = [], (e - a) // 2
        for gp in range(2):
            i = 0
            for part in (h, l):
                for cc in range(2):
                    lst.append((T[bank][:, n * gp:n * gp + n], MAT[(gp, cc)], T[part][:, a + cc:e:2], i == 0, i == 3))
                    i += 1
        return lst

    def codes(t, w):
        return T.land1[:, 64 * t:64 * t + 32] if w else T.land0[:, 16 * t:16 * t + 16]

    COL = (slice(0, 16), slice(16, 48))

    def arr_s(t, w):
        act(T.LA[:, COL[w]], codes(t, w), ACT.Copy, "land%d_%d" % (t, w), "LA%d" % w, bias=1184.0)
        act(T.Lh[:, COL[w]], T.LA[:, COL[w]], ACT.Copy, "LA%d" % w, "Lh%d" % w)

    def arr_u(t, w):
        ts(T.Lu[:, COL[w]], codes(t, w), float(PAD), None, OP.add, None, "land%d_%d" % (t, w), "Lu%d" % w)

    def arr_l(w):
        tt(T.Ll[:, COL[w]], T.LA[:, COL[w]], T.Lh[:, COL[w]], OP.subtract, "LA%d Lh%d" % (w, w), "Ll%d" % w)
        mms(conv("Lh", "Ll", "MS", 16, 48) if w else conv("Lh", "Ll", "MS"), "Lh%d Ll%d Ev Od" % (w, w), "MS")

    def arr_e(w):
        if not w:
            act(T.LS[:, 0:16], T.MS[:, 0:16], ACT.Copy, "", "MS LS0")
        for k in (1, 2) if w else ():
            for gp in range(2):
                act(T.LS[:, 16 * k + 8 * gp:16 * k + 8 * gp + 8], T.MS[:, 16 * gp + 8 * k - 8:16 * gp + 8 * k], ACT.Copy,
                    "", "MS LS%d" % k)

    def masks1(t):
        act(T.n12[:], T.land1[:, 64 * t + 32:64 * t + 64], ACT.Relu, "land%d_1" % t, "n12", scale=-1.0)
        act(T.u1[:], T.n12[:, 0:16], ACT.Copy, "n12", "u1", scale=-BIG, bias=BIG)

    def masks2(t):
        IN, lk = T.land1[:, 64 * t + 48:64 * t + 64], "land%d_1" % t
        act(T.s21[:], IN, ACT.Relu, lk, "s21")
        act(T.u2[:], T.s21[:], ACT.Copy, "s21", "u2", scale=BIG)
        act(T.a2[:], IN, ACT.Abs, lk, "a2")
        act(T.s20[:], T.a2[:], ACT.Copy, "a2", "s20", scale=-1.0, bias=1.0)
        for k in (1, 2):
            act(T.LAk[:, 16 * k - 16:16 * k], kk("LA", k), ACT.Copy, "LA1", "LAk%d" % k, scale=-32.0, bias=32.0 * k)

    def npart(t, k, bs, btok):
        es = btok == "Es"
        w0 = 77 * t - REM[t]

        def nu(gp):
            return lambda: ts(T.nu[:, gp::2], T.nn[:, 8 * gp:8 * gp + 8], T.nc[:, 2 * t + gp:2 * t + gp + 1], None, OP.add,
                              None, "nn nc%d" % (2 * t + gp), "nu%d" % gp)

        def ctu(ch):
            return lambda: cp(T.CTu[:, 64 * ch:64 * ch + 64], T.CT[:, ch::4], "CT", "CTu%d" % ch)
        return [
            lambda: tt(T.z32[:], kk("LS", k), bs, OP.mult, "LS%d" % k + (" Es" if es else ""), "z32" + ("" if es else " CV")),
            lambda: ts(T.nn[:], T.z32[:], 5, 1023, OP.arith_shift_right, OP.bitwise_and, "z32", "nn"),
            nu(0), nu(1),
            lambda: ts(T.C[:], T.FA[:, w0:2 * FW].indirect(T.nu[:]), float(PAD), None, OP.add, None,
                       "nu0 nu1 FAx0 FAx1 " + FAtok, "C"),
            lambda: op("v", lambda e: e.transpose(out=T.CT[:], in_=T.C[:]), "C", "CT"),
            ctu(3), ctu(0), ctu(1), ctu(2)]

    def xl(k, halves=(slice(0, 16),)):
        for s in halves:
            act(T.XL[:, 256 * k + 16 * s.start:256 * k + 16 * s.stop], Xw.indirect(T.Lu[:, 16 * k + s.start:16 * k + s.stop]),
                ACT.Copy, "X Xpad Lu%d" % min(k, 1), "XL%d_%d" % (k, s.start))

    HALVES = (slice(0, 8), slice(8, 16))

    def qpart(k, off, otok, halves=(slice(0, 16),)):
        for s in halves:
            a, e = 16 * s.start, 16 * s.stop
            tt(T.qq[:, a:e], Xw.indirect(off[:, s]), T.XL[:, 256 * k + a:256 * k + e], OP.max,
               "X Xpad %s XL%d_%d" % (otok, k, s.start), "qq1" if a else ("qq0" if e < 256 else "qq0 qq1"))
        for h in range(2):
            act(T.Q4[:, 512 * h:512 * h + 512], T.qq[:, 128 * h:128 * h + 128].indirect(T.EXu[:]), ACT.Copy,
                "qq%d EXu" % h, "Q4%d" % h)

    PLACE = {ch: ("DA", T.DA[:, ch:256:4]) for ch in (0, 1, 3)}
    PLACE[2] = ("DB", T.DB[:, 0:64])

    def starts():
        mms([(T.DA[:, 0:256], T.I32[:], T.CT[:], True, False),
             (T.DA[:, 0:256], T.oneb[0:1, :], T.MK[0:1, :], False, False)], "CT I32 oneb MK", "DA")
        mms([(T.DB[:, 0:64], T.I32[:], T.CT[:, 2::4], True, False),
             (T.DB[:, 0:64], T.oneb[0:1, :], T.MK2[0:1, :], False, False)], "CT I32 oneb MK2", "DB")

    def sums(ch, ps, last, r):
        tok, d = PLACE[ch]
        mms([(d, T.W65[:, 15 - p:143 - p], T["z%d" % ch][:, p::16], False, last and p == ps[-1]) for p in ps], r + " W65", tok)

    def fused(ch, h, w):
        a, b, q = (0, 64, "Q40 Q41") if h is None else (32 * h, 32 * h + 32, "Q4%d" % h)
        tt(T["z%d" % ch][:, 16 * a:16 * b], Xw.indirect(T.CTu[:, 64 * ch + a:64 * ch + b]),
           T.Q4[:, 16 * a:16 * b], OP.subtract, "X Xpad CTu%d %s" % (ch, q), w)

    def absz(a, tok):
        act(a, a, ACT.Abs, tok, tok)

    ALL = list(range(16))

    def pair(ch, toks):
        z = T["z%d" % ch]
        for s in range(2):
            absz(z[:, s::2], toks[s])
            sums(ch, ALL[s::2], s == 1 and ch == 1, toks[s])

    def main():
        for h in range(2):
            act(T.z3[:, 512 * h:512 * h + 512], Xw.indirect(T.CTu[:, 192 + 32 * h:224 + 32 * h]), ACT.Copy,
                "X Xpad CTu3", "z3e%d z3o%d" % (h, h))
        starts()
        for h in range(2):
            mms([(T.q4ps[:, 512 * h:512 * h + 512], T.IB[:], T.Q4[:, 512 * h:512 * h + 512], True, True)], "IB Q4%d" % h, "qp%d" % h)
        fused(0, 0, "z0e z0o")
        fused(0, 1, "z0e z0o")
        pair(0, ("z0e", "z0o"))
        for h in range(2):
            z, tok = T.z3[:, 512 * h:512 * h + 512], "z3e%d z3o%d" % (h, h)
            tt(z, z, T.q4ps[:, 512 * h:512 * h + 512], OP.subtract, tok, tok + " qp%d" % h)
        pair(3, ("z3e0 z3e1", "z3o0 z3o1"))
        fused(1, None, "z1e z1o")
        pair(1, ("z1e", "z1o"))
        fused(2, 0, "z2a")
        absz(T.z2[:, 0:512], "z2a")
        fused(2, 1, "z2e z2o")
        absz(T.z2[:, 512::2], "z2e")
        sums(2, ALL[0::2], False, "z2a z2e")
        absz(T.z2[:, 513::2], "z2o")
        sums(2, ALL[1::2], True, "z2a z2o")

    def scan(b):
        op("v", lambda e: e.tensor_tensor_scan(out=T["S" + b][:], data0=T["RS" + b][:], data1=T["D" + b][:, 0:256 if b == "A" else 64],
                                               initial=BIG, op0=OP.max, op1=OP.min), "RS" + b, "S%s D%s" % (b, b))

    MA, MB = T.SA[:, 15::16], T.SB[:, 3::4]

    def chain(k):
        tt(T.t1[:], T.Mu[:], MB, OP.min, "Mu SB", "t1")
        tt(T.t2[:], T.t1[:], T["w%d" % k][:], OP.max, "t1 w%d" % k, "t2")
        ts(T.bi[:], T.t2[:], 4095, None, OP.bitwise_and, None, "t2", "bi")
        cp(T.bh[:], T.bi[:], "bi", "bh")
        cp(T.bu[:], T.bi[:], "bi", "bu")
        tt(T.bl[:], T.bi[:], T.bh[:], OP.subtract, "bi bh", "bl")
        mms(conv("bh", "bl", "CV"), "bh bl Ev Od", "CV")
        qpart(k, T.bu, "bu")

    def keys(k):
        tc = T.Tk[:, k:k + 1]
        r = [lambda: tt(kk("K", k), MA, MB, OP.min, "SA SB", "K%d" % k),
             lambda: ts(kk("B", k), kk("K", k), 4095, None, OP.bitwise_and, None, "K%d" % k, "B%d" % k)]
        if k == 0:
            r.append(lambda: ts(kk("lv", 0), kk("K", 0), tc, None, OP.is_lt, None, "K0 Tk", "lv0"))
        else:
            r.append(lambda: ts(T.lt[:], kk("K", k), tc, None, OP.is_lt, None, "K%d Tk" % k, "lt"))
            r.append(lambda: tt(kk("lv", k), T.lt[:], T["g%d" % k][:], OP.mult, "lt g%d" % k, "lv%d" % k))
        r.append(lambda: tt(T.yo[:], kk("B", k), kk("lv", k), OP.mult, "B%d lv%d" % (k, k), "yo"))
        r.append(lambda: cp(kk("yu", k), T.yo[:], "yo", "yu%d" % k))
        return r

    def send(t, w, src, dst_ap):
        dst = T.cores[(rank + 1) % n_ranks if t < NV - 1 else (rank - t) % n_ranks]
        before("g", ["src%d_%d" % (t, w)], [])
        rid, pid = topo.addr(dst, core)
        ar = "ar%d_%d" % (t + 1, w)
        g.remote_dma(dst_ap, src, T.sem[ar], T.sem.ls, pid, rid, topo.mask(core, dst))
        ne = len(topo.engines(core, dst))
        sent[0] += ne
        lastw["land%d_%d" % (t + 1, w)] = (ar, ne, "remote")

    def rewire0_pre(t):
        tt(T.rz0[:], kk("LA", 0), T.Er[:], OP.mult, "LA0 Er", "rz0")
        ts(T.NW0[:], T.rz0[:], 5, 2047, OP.arith_shift_right, OP.bitwise_and, "rz0", "NW0")
        tt(T.df0[:], T.NW0[:], T.land0[:, 16 * t:16 * t + 16], OP.subtract, "NW0 land%d_0" % t, "df0")

    def rewire0(t):
        tt(T.x0[:], T.df0[:], kk("lv", 0), OP.mult, "df0 lv0", "x0")
        src = T.src0[:, 16 * t:16 * t + 16]
        tt(src, T.NW0[:], T.x0[:], OP.subtract, "NW0 x0", "src%d_0" % t)
        send(t, 0, src, T.land0[:, 16 * t + 16:16 * t + 32])

    def rewire1_p1():
        return [lambda: tt(T.px[:], kk("B", 0), T.Ep[:], OP.subtract, "B0 Ep", "px"),
                lambda: tt(T.px[:], T.px[:], kk("lv", 0), OP.mult, "px lv0", "px"),
                lambda: ts(T.NW[:, 32:48], kk("lv", 0), -1.0, None, OP.add, None, "lv0", "NWp1"),
                lambda: tt(T.P12[:, 0:16], T.px[:], T.Ep[:], OP.add, "px Ep", "P1")]

    def rewire1_pre(t):
        return [lambda: tt(T.qx[:], kk("B", 1), T.P12[:, 0:16], OP.subtract, "B1 P1", "qx"),
                lambda: tt(T.qx[:], T.qx[:], kk("lv", 1), OP.mult, "qx lv1", "qx"),
                lambda: tt(T.P12[:, 16:32], T.qx[:], T.P12[:, 0:16], OP.add, "qx P1", "P2"),
                lambda: tt(T.NW[:, 48:64], T.pa[:], T.pb[:], OP.max, "pa pb", "NWp2"),
                lambda: tt(T.rz12[:], T.LA[:, 16:48], T.P12[:], OP.mult, "LA1 P1 P2", "rz12"),
                lambda: tt(T.rk12[:], T.rz12[:], T.LAk[:], OP.add, "rz12 LAk1 LAk2", "rk12"),
                lambda: ts(T.NW[:, 0:32], T.rk12[:], 5, 2047, OP.arith_shift_right, OP.bitwise_and, "rk12", "NWl"),
                lambda: tt(T.df[:], T.NW[:], T.land1[:, 64 * t:64 * t + 64], OP.subtract, "NWl NWp1 NWp2 land%d_1" % t, "df")]

    def rewire1(t):
        src = T.src1[:, 64 * t:64 * t + 64]
        return [lambda: tt(T.xx[:], T.df[:], T.lvd[:], OP.mult, "df lvd0 lvd1", "xx"),
                lambda: tt(src, T.NW[:], T.xx[:], OP.subtract, "NWl NWp1 NWp2 xx", "src%d_1" % t),
                lambda: send(t, 1, src, T.land1[:, 64 * t + 64:64 * t + 128])]

    def thresholds():
        return [lambda: op("v", lambda e: e.tensor_reduce(out=T.cnt[:], in_=T.CV[:, 0:48], axis=AxisListType.X, op=OP.add), "", "cnt CV"),
                lambda: ts(T.ai[:], T.cnt[:], -1.0, 6144.0, OP.mult, OP.add, "cnt", "ai"),
                lambda: ts(T.ai2[:], T.ai[:], 31, None, OP.bitwise_and, None, "ai", "ai2"),
                lambda: ts(T.af[:], T.ai2[:], 65536.0, None, OP.mult, None, "ai2", "af"),
                lambda: ts(T.Tk[:], T.thk[:], T.af[:], None, OP.add, None, "thk af", "Tk")]

    ts(T.Ep[:], T.exi[:], float(PAD), None, OP.add, None, "exi", "Ep")
    cp(T.eh[:], T.Ep[:], "Ep", "eh")
    tt(T.el[:], T.Ep[:], T.eh[:], OP.subtract, "Ep eh", "el")
    mms(conv("eh", "el", "CV"), "eh el Ev Od", "CV")
    act(T.Es[:], T.CV[:, 0:16], ACT.Copy, "", "CV Es")
    cp(T.land0[:, 0:16], T.lci[:, 0:16], "lci", "land0_0")
    cp(T.Eu[:], T.Ep[:], "Ep", "Eu")
    arr_s(0, 0)
    arr_u(0, 0)
    arr_l(0)
    arr_e(0)
    xl(0, HALVES)
    cp(T.Er[:], T.exi[:], "exi", "Er")
    ts(T.W65[:], T.W[:], 65536.0, None, OP.mult, None, "W", "W65")
    cp(T.IB[:], T.I32[:], "I32", "IB")
    ts(T.RSA[:], T.RSA[:], BIG, None, OP.mult, None, "RSA", "RSA")
    ts(T.RSB[:], T.RSB[:], BIG, None, OP.mult, None, "RSB", "RSB")
    fill(T.MK[0:1, 2::4], BIG, "MK")
    np_ = npart(0, 0, T.Es[:], "Es")
    weave(np_[0:4], [])
    qpart(0, T.Eu, "Eu", HALVES)
    cp(T.land1[:, 0:32], T.lci[:, 16:48], "lci", "land0_1")
    ts(T.tsel[:], T.tsel[:], 65536.0, None, OP.mult, None, "tsel", "tsel")
    ts(T.base[:], T.b128[:], T.p8[:], None, OP.add, None, "b128 p8", "base")
    fill(T.mone[:], -1.0, "mone")
    dma("y", T.yi[:, 0:16], T.mone[:], "dout", 64, "mone", "yi0")
    weave(np_[4:], [])
    cp(T.land1[:, 32:64], T.upi[:, 16:48], "upi", "land0_1")
    cp(T.thf[:], T.thi[:], "thi", "thf")
    cp(T.wtf[:], T.wti[:], "wti", "wtf")
    ts(T.SW[:], T.W[:], T.wtf[:], None, OP.mult, None, "W wtf", "SW")
    for b in range(2):
        dma("y", T.FA[:, b * FW + 1024:(b + 1) * FW], T.FA[:, b * FW:b * FW + FW - 1024], "dfw", 32, FAtok, "FAx%d" % b)

    for t in range(NV):
        more = t < NV - 1
        main()
        if t == 0:
            mms([(T.MS[:, 0:3], T.tsel[:], T.thf[:], True, True)], "tsel thf", "MS")
            act(T.thk[:], T.MS[:, 0:3], ACT.Copy, "", "MS thk")
            act(T.Tk[:], T.thk[:], ACT.Copy, "thk", "Tk")
        arr_u(t, 1)
        arr_s(t, 1)
        masks1(t)
        xl(1)
        rewire0_pre(t)
        scan("A")
        arr_l(1)
        masks2(t)
        arr_e(1)
        tt(T.w1[:], T.n12[:, 0:16], T.Ep[:], OP.mult, "n12 Ep", "w1")
        tt(T.Mu[:], MA, T.u1[:], OP.min, "SA u1", "Mu")
        tt(T.nE[:], T.n12[:, 16:32], T.Ep[:], OP.mult, "n12 Ep", "nE")
        scan("B")
        chain(1)
        ks = keys(0)
        weave(ks[0:2], [])
        weave(npart(t, 1, T.CV[:, 0:16], "CV"), ks[2:])
        main()
        xl(2)
        act(T.y0[:], Xw.indirect(kk("yu", 0)), ACT.Copy, "X Xpad yu0", "y0")
        rewire0(t)
        tt(T.sB[:], T.s20[:], kk("B", 0), OP.mult, "s20 B0", "sB")
        scan("A")
        weave([lambda: tt(T.w2[:], T.sB[:], T.nE[:], OP.add, "sB nE", "w2"),
               lambda: tt(T.Mu[:], MA, T.u2[:], OP.min, "SA u2", "Mu"),
               lambda: tt(T.g1[:], T.n12[:, 0:16], kk("lv", 0), OP.max, "n12 lv0", "g1"),
               lambda: tt(T.ga[:], T.s20[:], kk("lv", 0), OP.mult, "s20 lv0", "ga")], rewire1_p1())
        scan("B")
        chain(2)
        ks = keys(1)
        weave(ks[0:2], [])
        weave(npart(t, 2, T.CV[:, 0:16], "CV"), ks[2:])
        main()
        if more:
            arr_u(t + 1, 0)
            arr_s(t + 1, 0)
        act(T.pb[:], kk("lv", 0), ACT.Copy, "lv0", "pb", bias=-1.0)
        act(T.pa[:], kk("lv", 1), ACT.Copy, "lv1", "pa", scale=2.0, bias=-1.0)
        tt(T.gb[:], T.s21[:], kk("lv", 1), OP.mult, "s21 lv1", "gb")
        tt(T.ga[:], T.ga[:], T.n12[:, 16:32], OP.max, "ga n12", "ga")
        tt(T.y01[:], Xw.indirect(kk("yu", 1)), T.y0[:], OP.max, "X Xpad yu1 y0", "y01")
        scan("A")
        weave([lambda: tt(T.g2[:], T.ga[:], T.gb[:], OP.max, "ga gb", "g2"),
               (lambda: (arr_l(0), arr_e(0))) if more else None], rewire1_pre(t))
        scan("B")
        np_ = npart(t + 1, 0, T.Es[:], "Es") if more else []
        weave(keys(2), [None] * 3 + np_[0:4])
        for h in range(2):
            act(T.lvd[:, 32 * h:32 * h + 32], T.lv[:, 16:48], ACT.Copy, "lv1 lv2", "lvd%d" % h)
        tt(T.yy[:], Xw.indirect(kk("yu", 2)), T.y01[:], OP.max, "X Xpad yu2 y01", "yy")
        mms([(T.CV[:, 0:16], T.SW[:, 15 - p:143 - p], T.yy[:, p::16], p == 0, p == 15) for p in ALL], "SW yy", "CV")
        weave(np_[4:], [])
        put = [lambda: cp(T.si[:], T.CV[:, 0:16], "", "si CV"),
               lambda: ts(T.sm[:], T.si[:], 7, None, OP.bitwise_and, None, "si", "sm"),
               lambda: tt(T.sa[:], T.sm[:], T.base[:], OP.add, "sm base", "sa")]
        if more:
            put.append(lambda: cp(T.wu[:], T.sa[:], "sa", "wu"))
            weave(put, rewire1(t))
            op("v", lambda e: e.tensor_copy(out=Xw.indirect(T.wu[:]), in_=T.yy[:]), "wu yy", "X Xpad")
            xl(0, HALVES)
            mms([(T.CV[:, 0:48], T.oneb[:], T.lv[:], True, True)], "oneb lv0 lv1 lv2", "CV")
            th = thresholds()
            weave(th[0:3], [])
            qpart(0, T.Eu, "Eu", HALVES)
            weave(th[3:], [])
        else:
            weave(rewire1(t), put)
            M = PAD + 1024
            cp(T.wu[:, 0:8], T.sa[:, 0:8], "sa", "wu0")
            ts(T.wu[:, 8:16], T.sa[:, 8:16], float(-M), None, OP.add, None, "sa", "wu1")
            op("v", lambda e: e.tensor_copy(out=T.X[:, 0:M].indirect(T.wu[:, 0:8]), in_=T.yy[:, 0:128]), "wu0 yy X", "Xpad")
            op("v", lambda e: e.tensor_copy(out=T.X[:, M:M + 1024].indirect(T.wu[:, 8:16]), in_=T.yy[:, 128:256]), "wu1 yy", "X")
            dma("s", T.yx[:, 0:1024], T.X[:, PAD:M], "dy", 32, "Xpad", "yxo0")
            dma("s", T.yx[:, 1024:2048], T.X[:, M:M + 1024], "dy", 32, "X", "yxo1")

    dma("y", T.yl[:, 0:16], T.land0[:, 16 * NV:16 * NV + 16], "dout", 64, "land%d_0" % NV, "ylo0")
    dma("y", T.yl[:, 16:48], T.land1[:, 64 * NV:64 * NV + 32], "dout", 64, "land%d_1" % NV, "ylo1")
    dma("y", T.yi[:, 16:48], T.land1[:, 64 * NV + 32:64 * NV + 64], "dout", 64, "land%d_1" % NV, "yio1")
    need("g", "dout", 64)
    need("g", "dy", 32)
    need("g", "ls", sent[0])
    for q in ("v", "s", "p", "g"):
        need("g", "c" + q, count[q])
